import numpy as np, ml_dtypes
CORES = [5,29,101,125,133,157,229,253]
N = 8
BF = ml_dtypes.bfloat16
def gentries(a):
    return np.ascontiguousarray(a.reshape(8, 16, -1).transpose(0, 2, 1)).reshape(8, -1)
def gtable(e):
    e = np.asarray(e); return np.ascontiguousarray(e.reshape(8, -1, 16).transpose(0, 2, 1)).reshape(128, -1).astype(np.int32)
C, M, G, T, TH, S = 4096, 512, 256, 4, 11, 16
def parts(rng):
    R = rng.integers(0, 256, (N, 8, 16, C)); P = rng.integers(0, M, (N, 8, 16, M)); O = rng.integers(0, M, (N, 8, 16, M))
    z = (256 * rng.choice(np.array([0.6, 0.8, 1.0]), (N, 8, 1, G)) * rng.random((N, 8, 16, G))).astype(np.int64)
    return R, P, O, z, rng.integers(0, M, (N, 8, G)), rng.integers(1, 257, (N, 8, 16))
def pack(R, P, O, z, mv, w):
    P = np.array(P); O = np.array(O); P[:, :, 0] = np.arange(M); O[:, :, 0] = np.arange(M)
    return {"strat": R.reshape(N, 128, C).astype(np.float32).astype(BF), "vp": P.reshape(N, 128, M).astype(np.int32), "vo": O.reshape(N, 128, M).astype(np.int32),
            "z0": z.reshape(N, 128, G).astype(np.float32).astype(BF), "mv": np.stack([gtable(a) for a in mv]), "wt": w.reshape(N, 128, 1).astype(np.int32)}
def plant(rng, R, P, O, z, mv, w):
    h = 17 - TH; m = np.arange(M)
    w[:, :, 13] = 16; w[:, :, 14] = 1; w[:, 2, :13] = np.maximum(w[:, 2, :13], 160)
    for r in range(N):
        q = (r + 1) % N
        for g in range(8):
            own = rng.permutation(M)[:12]; i = 1 + rng.permutation(G - 17)[:5]; wq = w[q, g]
            for e in range(4):
                a = int(i[e]); mv[r, g, a] = own[e]; P[r, g, 3 + 4 * e, own[e]] = M - 1
                z[r, g, :h, a] = 255; z[r, g, 13:15, a] = 0
                d = (4065 - int(np.sum(wq * z[r, g, :, a]))) & 4095
                z[r, g, 13, a] = d >> 4; z[r, g, 14, a] = d & 15
            if g == 2:
                left = 2 ** 19
                for j in list(range(13)) + [15, 13, 14]:
                    n = min(255, left // int(wq[j])); z[r, g, j, int(i[4])] = n; left -= n * int(wq[j])
            end = G - 15 + 2 * np.arange(8); mv[r, g, end] = own[4:]
            z[r, g, :h, G - 15::2] = 255
            u = np.sum(wq[:, None] * z[r, g], axis=0) & 4095; p0 = int(u[0]) & (S - 1)
            R[q, g, :, p0] = 255 * rng.integers(0, 2, 16)
            ad = (((m[:, None] * u[end][None, :]) >> 5) + m[:, None] + 37 * 15) & (C - 1)
            for e in range(8):
                good = np.flatnonzero(ad[:, e] == p0)
                if len(good): P[r, g, 15, own[4 + e]] = rng.choice(good)
    return R, P, O, z, mv, w
def setup_inputs(rng):
    return pack(*plant(rng, *parts(rng)))
def corner(rng, first):
    R, P, O, z, mv, w = parts(rng); R = np.maximum(R, 1); m = np.arange(M)[None, :]; j = np.arange(16)[:, None]
    forms = [m + 0 * j, np.maximum(m - j, 0), np.minimum(m + j, M - 1), np.where((m + j) % 2 == 0, 0, M - 1)]
    P = np.stack([np.stack([forms[(g + r) % 4] for g in range(8)]) for r in range(N)])
    O = np.stack([np.stack([forms[(g + r + 1 + g // 4) % 4] for g in range(8)]) for r in range(N)])
    cnt = np.array([255, 256, 1024, 512, 257, 511, 1, 8 * G - 1, 8 * G, 0, 1536, 4 * G, 6 * G, 8 * G - 256, 1023, 1025])[first * N:first * N + N]
    cnt = np.roll(cnt, int(rng.integers(0, N)))
    for r in range(N):
        for g in range(8):
            e = (g + r) % 3
            if e == 0: mv[r, g] = rng.choice(np.array([0, M - 1]), G)
            elif e == 1: mv[r, g] = rng.integers(0, M)
            else: mv[r, g] = rng.permutation(M)[:G]
        hit = np.zeros(8 * G, bool); hit[rng.permutation(8 * G)[:int(cnt[r])]] = True
        z[r] = np.where(hit.reshape(8, 1, G), 0, 255)
    w[:, 1] = 1; w[:, 5] = 256
    return pack(R, P, O, z, mv, w)
def setup_inputs_corners(rng):
    return corner(rng, 0)
def setup_inputs_corners_two(rng):
    return corner(rng, 1)
def setup_inputs_ends(rng):
    R = np.where(rng.random((N, 8, 16, C)) < rng.choice(np.array([0.1, 0.5, 0.75, 0.9]), (N, 8, 1, C)), 255, 0)
    z = np.where(rng.random((N, 8, 16, G)) < rng.choice(np.array([0.05, 0.3, 0.8]), (N, 8, 1, G)), 255, 0)
    P = (M - 1) * rng.integers(0, 2, (N, 8, 16, M)); O = (M - 1) * rng.integers(0, 2, (N, 8, 16, M)); mv = (M - 1) * rng.integers(0, 2, (N, 8, G))
    w = np.where(rng.random((N, 8, 16)) < 0.5, 256, 1)
    mv[:, :, G - 1] = M - 1; P[:, :, 15, M - 1] = M - 1; O[:, :, 15, M - 1] = M - 1
    w[:, 0] = 256; R[:, 0] = np.where(rng.random((N, 1, C)) < 0.5, 255, 0); z[:, 0, :, G - 1] = 255; z[:, 0, :, 0] = 0
    w[:, 5:] = 256; w[:, 5:, 15] = 1
    c = np.zeros(16, np.int64); c[3] = 255; c[15] = 255
    x8 = np.array([0, 1, 2, 4, 5, 6, 7, 8]); y4 = np.array([9, 10, 11, 12])
    for g in (6, 7):
        hot = ((np.arange(C) >> 7) + g) % 2 == 1
        R[:, g] = c[None, :, None]
        R[:, g, x8] = np.where(hot, 192, 64 * rng.integers(0, 2, (N, 1, C))); R[:, g, y4] = np.where(hot, 128, 0)
        z[:, g, :, 1::2] = c[None, :, None]; z[:, g, :, G - 1] = c[None, :]
    R[:, 5] = 0; R[:, 5, 15] = 255; R[:, 5, y4] = 128 * rng.integers(0, 2, (N, 1, C))
    R[:, 5, x8, C - 1] = 192; R[:, 5, y4, C - 1] = 128
    z[:, 5] = 0; z[:, 5, 15] = 255
    m = np.arange(M); f = ((m * 255) >> 5) + m
    for j in range(1, 14):
        near = m[((f + 37 * (j + 1)) & (C - 1)) >= C - 256]
        P[:, 5, j] = rng.choice(near, (N, M)); O[:, 5, j] = rng.choice(near, (N, M))
    P[:, 5, 14:] = rng.integers(0, M, (N, 2, M)); O[:, 5, 14:] = rng.integers(0, M, (N, 2, M))
    mv[:, 5] = np.argsort(rng.random((N, M)), axis=1)[:, :G]; mv[:, 5, G - 1] = M - 1
    keep = np.array(R[3, 5])
    z[1, :, :17 - TH] = 255; z[2, :, :TH] = 0; R[3, :, :TH] = 255
    a0 = f[mv[2, 5]] & (C - 1); keep[np.ix_(x8, a0)] = 192; keep[np.ix_(y4, a0)] = 128; R[3, 5] = keep
    return pack(R, P, O, z, mv, w)
def setup_inputs_spread(rng):
    R = np.minimum((np.exp2(8 * rng.random((N, 8, 1, C))) * rng.random((N, 8, 16, C))).astype(np.int64), 255)
    z = np.minimum((np.exp2(8 * rng.random((N, 8, 1, G))) * rng.random((N, 8, 16, G))).astype(np.int64), 255)
    P = np.minimum((M * rng.random((N, 8, 16, M)) ** 3).astype(np.int64), M - 1); O = np.minimum((M * rng.random((N, 8, 16, M)) ** 3).astype(np.int64), M - 1)
    mv = np.minimum((M * rng.random((N, 8, G)) ** 2).astype(np.int64), M - 1)
    w = np.minimum(np.maximum(np.rint(np.exp2(8 * rng.random((N, 8, 16)))).astype(np.int64), 1), 256)
    v0 = [v for v in range(M + G * (T - 2), M + G * (T - 1)) if (-(2 ** 22)) % v < 32][0]
    u0 = (2 ** 22 + v0 - 1) // v0 - 32
    r = int(rng.integers(0, N)); q = (r + 1 + (T - 1) % (N - 1)) % N; p = (r + 1 + (T - 2) % (N - 1)) % N
    R[q, :, :17 - TH] = 0
    for g in (1, 3, 4, 6):
        w[q, g, 13] = 16; w[q, g, 14] = 1
        c = rng.integers(0, 256, 16); c[13:15] = 0
        d = (u0 - int(np.sum(w[q, g] * c))) & 4095
        c[13] = d >> 4; c[14] = d & 15
        R[p, g] = c[:, None]
        R[q, g, 15] = 0; R[q, g, 15, 0] = 255
    return pack(R, P, O, z, mv, w)
def setup_inputs_ties(rng):
    R, P, O, z, mv, w = parts(rng)
    b = rng.integers(0, 255, (8, 16)); b[0] = 0; b[6] = 254
    share = rng.permutation(np.array([0.02, 0.04, 0.07, 0.1, 0.15, 0.2, 0.3, 0.5])).reshape(1, 8, 1, 1)
    cnt = np.where(rng.random((N, 8, 1, C)) < share, rng.choice(np.array([TH, TH, TH, TH + 1, 16]), (N, 8, 1, C)), rng.choice(np.array([TH - 1, TH - 1, TH - 1, 0]), (N, 8, 1, C)))
    R = b[None, :, :, None] + (np.argsort(rng.random((N, 8, 16, C)), axis=2) < cnt)
    z = b[None, :, :, None] + (rng.random((N, 8, 1, G)) < 0.125) + np.zeros((N, 8, 16, G), np.int64)
    return pack(R, P, O, z, mv, w)
def check_inputs(d):
    bad = []
    for k, lo, hi in (("strat", 0, 255), ("vp", 0, M - 1), ("vo", 0, M - 1), ("z0", 0, 255), ("mv", 0, M - 1), ("wt", 1, 256)):
        a = np.asarray(d[k]).astype(np.float64)
        if not (np.min(a) >= lo and np.max(a) <= hi): bad.append("range of " + k)
        elif np.any(a != np.floor(a)): bad.append("whole numbers in " + k)
    for k in ("vp", "vo"):
        if np.any(np.asarray(d[k]).reshape(-1, 8, 16, M)[:, :, 0] != np.arange(M)): bad.append("row 0 of the views in " + k)
    return bad
def reference(strat, vp, vo, z0, mv, wt):
    R = strat.astype(np.float32).astype(np.int32).reshape(N, 8, 16, C); z = z0.astype(np.float32).astype(np.int32).reshape(N, 8, 16, G)
    w = wt.astype(np.int32).reshape(N, 8, 16, 1); v = np.stack([gentries(a) for a in mv]).astype(np.int64)
    room = np.zeros((N, 8, 16, G * T), np.int32)
    views = [np.concatenate([a.astype(np.int32).reshape(N, 8, 16, M), room], axis=3) for a in (vp, vo)]
    count = np.zeros(N, np.int64); kk = np.arange(16)[None, None, :, None]; verdicts = np.zeros((N, 8, T, G), np.int64)
    for t in range(T):
        mover, other = views[t % 2], views[1 - t % 2]
        q = (np.arange(N) + 1 + t % (N - 1)) % N
        L = np.take_along_axis(mover, v[:, :, None, :], 3).astype(np.int64)
        u = np.add.reduce(w[q] * z, axis=2).astype(np.int64) & 4095
        ad = (((L * u[:, :, None, :]) >> 5) + L + 37 * kk + (count[q] & 255)[:, None, None, None]) & (C - 1)
        Y = np.take_along_axis(R[q], ad.reshape(N, 8, 1, 16 * G), 3).reshape(N, 8, 16, 16, G)
        hit = np.add.reduce((Y > z[:, :, :, None, :]).astype(np.int32), axis=2) >= TH
        hit[:, :, 15] = True
        kap = np.argmax(hit, axis=2)
        use = (kk <= kap[:, :, None, :])[:, :, None]
        z = (np.maximum.reduce(np.where(use, Y, 0), axis=3) + np.minimum.reduce(np.where(use, Y, 255), axis=3)) >> 1
        z = z.astype(np.int32)
        if t < T - 1:
            place = S * np.arange(G) + (u & (S - 1))
            for r in range(N):
                ix = np.repeat(place[r][:, None, :], 16, axis=1); mine = R[int(q[r])]
                np.put_along_axis(mine, ix, (np.take_along_axis(mine, ix, 2) + z[r]) >> 1, 2)
        count[q] = np.add.reduce((kap < 15).reshape(N, 8 * G).astype(np.int64), axis=1)
        named = np.take_along_axis(L, kap[:, :, None, :], 2)
        resumed = np.take_along_axis(other, named, 3)
        n0 = M + G * t; n = np.zeros((N, 8, 1, G), np.int64) + n0 + np.arange(G)
        mover[..., n0:n0 + G] = np.concatenate([n, L[:, :, :15]], axis=2)
        other[..., n0:n0 + G] = np.concatenate([n, resumed[:, :, :15]], axis=2)
        v = n[:, :, 0]; verdicts[:, :, t] = kap
    e = M + G * (T - 1)
    return {"yp": views[0][..., e:e + G].reshape(N, 128, G).astype(np.float32), "yo": views[1][..., e:e + G].reshape(N, 128, G).astype(np.float32),
            "yz": z.reshape(N, 128, G).astype(np.float32).astype(BF), "yk": verdicts.reshape(N, 8, T * G).astype(np.float32)}

@@ -1,0 +1,639 @@
+from concourse.mybir import AluOpType as A, ActivationFunctionType as F
+
+N, TURNS, H = 8, 4, 128
+RW = 4096 + 816
+GS = (64, 128)
+CUTS = (48, 88)
+KS = (9, 8)
+M35, M23 = 1.5 * 2.0 ** 35, 1.5 * 2.0 ** 23
+
+SCRATCH = {
+    "RT": ("sbuf", [128, RW], "bfloat16"),
+    "VP32": ("sbuf", [128, 512], "int32"), "VO32": ("sbuf", [128, 512], "int32"),
+    "MV32": ("sbuf", [128, 16], "int32"), "MV16": ("sbuf", [128, 16], "uint16"),
+    "Z0B": ("sbuf", [128, 256], "bfloat16"), "WT32": ("sbuf", [128, 1], "int32"), "WTF": ("sbuf", [128, 1], "float32"),
+    "PV": ("sbuf", [128, 512], "float16"), "OV": ("sbuf", [128, 512], "float16"),
+    "HL1": ("sbuf", [128, 256], "float16"), "HL3": ("sbuf", [128, 256], "float16"),
+    "HB2": ("sbuf", [128, 256], "float16"), "HB3": ("sbuf", [128, 256], "float16"), "L3I": ("sbuf", [128, 256], "float16"),
+    "MX": ("sbuf", [128, 2048], "bfloat16"), "MN": ("sbuf", [128, 2048], "bfloat16"),
+    "DIF": ("sbuf", [128, 128], "float32"), "DB": ("sbuf", [128, 128], "float32"), "JI": ("sbuf", [128, 128], "int32"),
+    "JS": ("sbuf", [128, 128], "int32"), "JM": ("sbuf", [128, 128], "int32"), "PI": ("sbuf", [128, 1], "int32"),
+    "PG": ("sbuf", [128, 1], "int32"), "PK": ("sbuf", [128, 1], "int32"), "COL": ("sbuf", [128, 16], "float32"),
+    "BLK": ("sbuf", [128, 128], "bfloat16"), "T0": ("sbuf", [128, 128], "bfloat16"), "T1": ("sbuf", [128, 128], "bfloat16"),
+    "IB": ("sbuf", [128, 128], "bfloat16"), "NIB": ("sbuf", [128, 128], "bfloat16"), "IH": ("sbuf", [128, 128], "float16"),
+    "NH": ("sbuf", [128, 128], "float16"), "B14": ("sbuf", [128, 128], "bfloat16"),
+    "BF": ("sbuf", [128, 128], "float16"), "S0": ("sbuf", [128, 128], "float16"), "WB": ("sbuf", [128, 128], "float16"),
+    "DLM": ("sbuf", [128, 128], "float16"), "SH1": ("sbuf", [128, 128], "float16"), "SH2": ("sbuf", [128, 128], "float16"),
+    "MK": ("sbuf", [128, 256], "float16"), "MB": ("sbuf", [128, 128], "float16"), "QH": ("sbuf", [128, 8], "float16"),
+    "QF": ("sbuf", [128, 8], "float32"), "QB": ("sbuf", [128, 8], "bfloat16"), "QBH": ("sbuf", [128, 8], "bfloat16"),
+    "Q8": ("sbuf", [128, 8], "bfloat16"), "R14": ("sbuf", [128, 128], "float32"), "ROW0": ("sbuf", [128, 128], "float16"),
+    "ROW1": ("sbuf", [128, 128], "float16"), "ONE": ("sbuf", [128, 128], "float16"), "C32": ("sbuf", [128, 128], "float16"),
+    "CU": ("sbuf", [128, 128], "float16"), "NF": ("sbuf", [128, 256], "float32"), "PB": ("sbuf", [128, 16], "int32"),
+    "PB0": ("sbuf", [128, 16], "int32"), "PLI": ("sbuf", [128, 16], "int32"), "PLA": ("sbuf", [128, 16], "int32"),
+    "PLB": ("sbuf", [128, 16], "int32"), "PL": ("sbuf", [128, 16], "uint16"),
+    "AI": ("sbuf", [128, 1], "int32"), "AJ": ("sbuf", [128, 1], "int32"),
+    "YKS": ("sbuf", [8, 1024], "float32"), "YPS": ("sbuf", [128, 256], "float32"), "YOS": ("sbuf", [128, 256], "float32"),
+    "YZS": ("sbuf", [128, 256], "bfloat16"),
+    "pU": ("psum", [128, 512], "float32"), "pZ0": ("psum", [128, 512], "float32"), "pZ1": ("psum", [128, 512], "float32"),
+    "pD0": ("psum", [128, 512], "float32"), "pD1": ("psum", [128, 512], "float32"), "pC": ("psum", [128, 512], "float32"),
+    "pR": ("psum", [128, 512], "float32"), "pW": ("psum", [128, 512], "float32"),
+    "MI": ("sbuf", [128, 2560], "float16"),
+    "MO": ("sbuf", [128, 2560], "float16"),
+}
+for _t in range(4):
+    SCRATCH["VI%d" % _t] = ("sbuf", [128, 512], "float16")
+    SCRATCH["TAB%d" % _t] = ("sbuf", [128, 512 + 256 * _t], "float32")
+    SCRATCH["NC%d" % _t] = ("sbuf", [128, 256], "float16")
+    SCRATCH["RUN%d" % _t] = ("sbuf", [128, 256], "bfloat16")
+    SCRATCH["KI%d" % _t] = ("sbuf", [128, 256], "bfloat16")
+ALIAS = {}
+for _c in range(2):
+    for _t in range(5):
+        ALIAS["MI%d%d" % (_t, _c)] = ("MI", 256 * (2 * _t + _c))
+        ALIAS["MO%d%d" % (_t, _c)] = ("MO", 256 * (2 * _t + _c))
+for _n, _w, _d in (("Y", 2048, "bfloat16"), ("B", 2048, "bfloat16"), ("HI", 2048, "bfloat16"), ("LO", 2048, "bfloat16"),
+                   ("U1", 128, "float32"), ("U2", 128, "bfloat16"), ("AT", 128, "int32"), ("AS", 128, "int32"), ("OF", 128, "uint16"),
+                   ("CM", 128, "bfloat16"), ("RN", 128, "bfloat16"), ("P", 128, "float16"), ("ZM", 256, "float16"), ("ZU", 128, "float32"),
+                   ("LS", 16, "uint16"), ("HG", 128, "float32"), ("SM", 128, "float32"), ("RY", 128, "int32"), ("RZ", 128, "int32"),
+                   ("ACC", 1, "float32"), ("C8", 128, "float16")):
+    SCRATCH[_n] = ("sbuf", [128, 2 * _w], _d)
+    for _c in range(2):
+        ALIAS["%s%d" % (_n, _c)] = (_n, _w * _c)
+
+SEMAPHORES = (["qg", "qt", "qv", "qs", "ls"] + ["d%d" % i for i in range(28)]
+              + ["m%d%d" % (t, c) for t in range(5) for c in range(2)] + ["v%d" % t for t in range(4)]
+              + ["h%d%d" % (t, c) for t in range(4) for c in range(2)] + ["y%d%d" % (t, c) for t in range(4) for c in range(2)] + ["w0", "w1"])
+
+
+def real(o):
+    if o[0] in ALIAS:
+        n, a = ALIAS[o[0]]
+        return (n, o[1] + a, o[2] + a) + tuple(o[3:])
+    return o
+
+
+def bits(m):
+    return bin(m).count("1")
+
+
+def relay_of(src, dst, n, near, topo):
+    if topo.may_write(src, dst):
+        return None
+    c = [x for x in topo.cores_of(src) if x != src and topo.may_write(x, dst)]
+    c = [x for x in c if (topo.die(x) == topo.die(src)) == near]
+    return c[n % len(c)]
+
+
+def messages(core, T, topo):
+    r = T.rank_of(core)
+    out = []
+
+    def add(sem, off, buf, a, b, n, near):
+        dst = T.cores[(r + off) % N]
+        buf, a, b = real((buf, a, b))
+        out.append((sem, dst, relay_of(core, dst, n, near, topo), buf, a, b))
+    for c in range(2):
+        add("m0%d" % c, 1, "MI0%d" % c, 0, 256, c, True)
+    add("v0", 1, "VI0", 0, 512, 0, False)
+    add("v1", 2, "VI1", 0, 512, 0, False)
+    add("v2", 3, "VI2", 0, 512, 1, False)
+    add("v3", 4, "VI3", 0, 512, 0, False)
+    for c in range(2):
+        add("h1%d" % c, 2, "HL1", 128 * c, 128 * c + 128, 0, False)
+        add("h0%d" % c, 4, "HL3", 128 * c, 128 * c + 128, 0, False)
+    for t in range(4):
+        for c in range(2):
+            add("m%d%d" % (t + 1, c), 1 if t < 3 else -4, "MI%d%d" % (t + 1, c), 0, 256, c, True)
+            if t < 2:
+                add("h%d%d" % (t + 2, c), 2, "HB%d" % (t + 2), 128 * c, 128 * c + 128, 0, False)
+            if t == 3:
+                add("w%d" % c, -4, "L3I", 128 * c, 128 * c + 128, 0, False)
+            add("y%d%d" % (t, c), -1 - t, "KI%d" % t, 128 * c, 128 * c + 128, c, False)
+    return out
+
+
+def mask_of(src, dst, topo):
+    return sum(1 << x for x in topo.engines(src, dst)[:8])
+
+
+def hand_on(g, core, T, topo):
+    own = [x for x in topo.cores_of(core) if T.rank_of(x) is not None]
+    n = 0
+    for rc in own:
+        for sem, dst, rel, buf, a, b in messages(rc, T, topo):
+            if rel == core:
+                g.wait_ge(T.sem[sem], bits(mask_of(rc, core, topo)))
+                m = mask_of(core, dst, topo)
+                rid, pid = topo.addr(dst, core)
+                g.remote_dma(T[buf][:, a:b], T[buf][:, a:b], T.sem[sem], T.sem.ls, pid, rid, m)
+                n += bits(m)
+    if n:
+        g.wait_ge(T.sem.ls, n)
+
+
+def rank_program(g, core, T, topo):
+    rank = T.rank_of(core)
+    if rank is None:
+        hand_on(g, core, T, topo)
+        return
+    Q = {"g": g, "t": g.tensor, "v": g.vector, "s": g.scalar, "d": g.sync}
+    cnt = {"g": 0, "t": 0, "v": 0, "s": 0}
+    known = {q: {} for q in Q}
+    acc, bank, used = {}, {}, {}
+    state = {"d": 0, "ls": 0}
+
+    def need(q, tok):
+        sem, val, clk = tok
+        k = known[q]
+        if k.get(sem, 0) < val:
+            Q[q].wait_ge(T.sem[sem], val)
+            k[sem] = val
+        for s2 in clk:
+            if k.get(s2, 0) < clk[s2]:
+                k[s2] = clk[s2]
+
+    def deps(q, reads, writes):
+        toks = []
+        for w, lst in ((False, reads), (True, writes)):
+            for nm, lo, hi in lst:
+                if nm[0] == "p":
+                    for q2 in bank.get(nm, {}):
+                        if q2 != q:
+                            toks.append(bank[nm][q2])
+                    continue
+                for lo2, hi2, w2, q2, tok in acc.get(nm, []):
+                    if lo < hi2 and lo2 < hi and (w or w2) and not (q2 == q and w and not w2 and q in cnt):
+                        toks.append(tok)
+        best = {}
+        for tok in toks:
+            if tok[0] not in best or best[tok[0]][1] < tok[1]:
+                best[tok[0]] = tok
+        for tok in sorted(best.values(), key=lambda x: -len(x[2])):
+            need(q, tok)
+
+    def note(q, reads, writes, tok):
+        for w, lst in ((False, reads), (True, writes)):
+            for nm, lo, hi in lst:
+                if nm[0] == "p":
+                    bank.setdefault(nm, {})[q] = tok
+                    continue
+                l = acc.setdefault(nm, [])
+                if w:
+                    l[:] = [e for e in l if not (lo <= e[0] and e[1] <= hi)]
+                l.append((lo, hi, w, q, tok))
+
+    def op(q, fn, args, reads, writes):
+        deps(q, reads, writes)
+        fn(**args).then_inc(T.sem["q" + q], 1)
+        cnt[q] += 1
+        used["q" + q] = cnt[q]
+        note(q, reads, writes, ("q" + q, cnt[q], dict(known[q])))
+
+    def dma(q, out, in_, reads, writes):
+        deps(q, reads, writes)
+        s = "d%d" % state["d"]
+        state["d"] += 1
+        Q[q].dma_start(out, in_).then_inc(T.sem[s], 16)
+        used[s] = 16
+        note(q, reads, writes, (s, 16, dict(known[q])))
+
+    def arrives(sem, src_off, buf, a, b):
+        src = T.cores[(rank + src_off) % N]
+        for s2, dst, rel, bf, _a, _b in messages(src, T, topo):
+            if s2 == sem and dst == core:
+                v = bits(mask_of(rel if rel is not None else src, core, topo))
+                used[sem] = v
+                note("x", [], [real((buf, a, b))], (sem, v, {}))
+
+    plan = {m[0]: m for m in messages(core, T, topo)}
+
+    def send(sem, buf, a, b):
+        _, dst, rel, ob, oa, oe = plan[sem]
+        buf, a, b = real((buf, a, b))
+        deps("g", [(buf, a, b)], [])
+        to = dst if rel is None else rel
+        m = mask_of(core, to, topo)
+        rid, pid = topo.addr(to, core)
+        g.remote_dma(T[ob][:, oa:oe], T[buf][:, a:b], T.sem[sem], T.sem.ls, pid, rid, m)
+        state["ls"] += bits(m)
+
+    def ap(o):
+        o = real(o)
+        if len(o) == 4:
+            return T[o[0]][:, o[1]:o[2]:o[3]]
+        return T[o[0]][:, o[1]:o[2]]
+
+    def rg(o):
+        return real(o)[:3]
+
+    def ind(win, off):
+        return ap(win).indirect(ap(off))
+
+    def full(n, w=128):
+        return (n, 0, w)
+
+    def mm(out, l, r, start, stop):
+        op("t", g.tensor.matmul, dict(out=ap(out), lhsT=ap(l), rhs=ap(r), start=start, stop=stop), [rg(l), rg(r)], [rg(out)])
+
+    def mm1(out, l, r, start, stop):
+        op("t", g.tensor.matmul, dict(out=ap(out), lhsT=T[l[0]][0:1, l[1]:l[2]], rhs=T[r[0]][0:1, r[1]:r[2]], start=start, stop=stop), [rg(l), rg(r)], [rg(out)])
+
+    def tt(out, a, b, o):
+        op("v", g.vector.tensor_tensor, dict(out=ap(out), in0=ap(a), in1=ap(b), op=o), [rg(a), rg(b)], [rg(out)])
+
+    def tti(out, win, off, b, o):
+        op("v", g.vector.tensor_tensor, dict(out=ap(out), in0=ind(win, off), in1=ap(b), op=o), [rg(win), rg(off), rg(b)], [rg(out)])
+
+    def ts(out, a, s1, o1, s2=None, o2=None):
+        rd = [rg(a)]
+        sc = []
+        for s in (s1, s2):
+            if isinstance(s, tuple):
+                rd.append(rg(s))
+                sc.append(ap(s))
+            else:
+                sc.append(s)
+        d = dict(out=ap(out), in0=ap(a), scalar1=sc[0], scalar2=sc[1], op0=o1)
+        if o2 is not None:
+            d["op1"] = o2
+        op("v", g.vector.tensor_scalar, d, rd, [rg(out)])
+
+    def tc(out, a):
+        op("v", g.vector.tensor_copy, dict(out=ap(out), in_=ap(a)), [rg(a)], [rg(out)])
+
+    def ms(out, v):
+        op("v", g.vector.memset, dict(ap=ap(out), constant=v), [], [rg(out)])
+
+    def act(out, a, f, bias=None, scale=None, accum=None):
+        d = dict(out=ap(out), in_=ap(a), func=f)
+        wr = [rg(out)]
+        if bias is not None:
+            d["bias"] = bias
+        if scale is not None:
+            d["scale"] = scale
+        if accum is not None:
+            d["accum_out"] = ap(accum)
+            wr.append(rg(accum))
+        op("s", g.scalar.activation, d, [rg(a)], wr)
+
+    def acti(out, win, off, f, bias=None, scale=None):
+        d = dict(out=ap(out), in_=ind(win, off), func=f)
+        if bias is not None:
+            d["bias"] = bias
+        if scale is not None:
+            d["scale"] = scale
+        op("s", g.scalar.activation, d, [rg(win), rg(off)], [rg(out)])
+
+    dma("d", T.VP32[:], T.vp[:], [], [("VP32", 0, 512)])
+    dma("s", T.MV32[:], T.mv[:], [], [("MV32", 0, 16)])
+    dma("s", T.Z0B[:], T.z0[:], [], [("Z0B", 0, 256)])
+    dma("d", T.VO32[:], T.vo[:], [], [("VO32", 0, 512)])
+    dma("s", T.WT32[:], T.wt[:], [], [("WT32", 0, 1)])
+    dma("s", T.RT[:, 0:4096], T.strat[:], [], [("RT", 0, 4096)])
+    dma("d", T.RT[:, 4096:RW], T.strat[:, 0:RW - 4096], [], [("RT", 4096, RW)])
+
+    big = dict(allow_small_or_imprecise_dtypes=True)
+    op("g", g.iota, dict(out=T.PI[:], pattern=[[0, 1]], base=0, channel_multiplier=1), [], [("PI", 0, 1)])
+    op("g", g.iota, dict(out=T.JI[:], pattern=[[1, 128]], base=0, channel_multiplier=0), [], [("JI", 0, 128)])
+    op("g", g.iota, dict(out=T.DIF[:], pattern=[[1, 128]], base=0, channel_multiplier=-1, **big), [], [("DIF", 0, 128)])
+    op("g", g.iota, dict(out=T.PB0[:], pattern=[[0, 2], [256, 8]], base=0, channel_multiplier=0), [], [("PB0", 0, 16)])
+    op("g", g.iota, dict(out=T.NF[:], pattern=[[1, 256]], base=512, channel_multiplier=0, **big), [], [("NF", 0, 256)])
+
+    GP, KK, P16, K0, K14, KL, K37, E16, AK = [("COL", i, i + 1) for i in range(9)]
+    ts(full("PG", 1), full("PI", 1), 4, A.arith_shift_right)
+    ts(full("PK", 1), full("PI", 1), 15, A.bitwise_and)
+    ts(full("JS"), full("JI"), 4, A.arith_shift_right)
+    tc(GP, full("PG", 1))
+    tc(KK, full("PK", 1))
+    ts(K37, KK, 37.0, A.mult)
+    ts(full("BLK"), full("JS"), GP, A.is_equal)
+    ts(full("IH"), full("DIF"), 0.0, A.is_equal, 0.5, A.mult)
+    ts(full("T1"), full("BLK"), 1000.0, A.mult, 1000.0, A.subtract)
+    ms(full("ONE"), 1.0)
+    ms(full("C32"), 0.25)
+    tt(full("DB"), full("DIF"), full("T1"), A.add)
+    op("v", g.vector.memset, dict(ap=T.CU[0:64, :], constant=-32.0), [], [("CU", 0, 64)])
+    op("v", g.vector.memset, dict(ap=T.CU[64:128, :], constant=0.0078125), [], [("CU", 64, 128)])
+    ts(full("T0"), full("DB"), -1.0, A.is_equal)
+    ts(full("IB"), full("DIF"), 0.0, A.is_equal)
+
+    tc(full("MV16", 16), full("MV32", 16))
+    for c in range(2):
+        mo, off = "MO0%d" % c, ("MV16", 8 * c, 8 * c + 8)
+        tc((mo, 0, 128), ("Z0B", 128 * c, 128 * c + 128))
+        op("v", g.vector.tensor_copy, dict(out=ap((mo, 128, 256)), in_=ind(("VP32", 0, 512), off)), [("VP32", 0, 512), off], [rg((mo, 128, 256))])
+        send("m0%d" % c, mo, 0, 256)
+    tt(full("DLM"), full("T0"), full("IB"), A.subtract)
+    ts(full("NIB"), full("DIF"), 0.0, A.is_equal, -1.0, A.mult)
+    tc(full("OV", 512), full("VO32", 512))
+    send("v0", "OV", 0, 512)
+    tc(full("WTF", 1), full("WT32", 1))
+    ts(full("WB"), full("BLK"), full("WTF", 1), A.mult)
+    tc(full("PV", 512), full("VP32", 512))
+    send("v1", "PV", 0, 512)
+    for c in range(2):
+        send("h1%d" % c, "MO0%d" % c, 128, 256)
+    send("v2", "OV", 0, 512)
+    send("v3", "PV", 0, 512)
+    for c in range(2):
+        send("h0%d" % c, "MO0%d" % c, 128, 256)
+
+    def const_a():
+        ts(full("NH"), full("DIF"), 0.0, A.is_equal, -0.5, A.mult)
+        ts(full("JM"), full("JI"), 15, A.bitwise_and)
+        ts(full("QB", 8), ("JI", 0, 8), GP, A.is_equal)
+        ts(full("QBH", 8), ("JI", 0, 8), GP, A.is_equal, 0.5, A.mult)
+        for c in range(2):
+            ts(full("C8%d" % c), full("JM"), KS[c] - 0.5, A.is_gt, 0.0625, A.mult)
+        ms(full("MX", 2048), 1.0)
+        op("v", g.vector.memset, dict(ap=T.MX[:, 0:2048:16], constant=0.0), [], [("MX", 0, 2048)])
+        ts(KL, KK, 15.0, A.is_lt)
+        ts(K0, KK, 0.0, A.is_equal)
+        ts(P16, full("PI", 1), 16.0, A.mult)
+        ts(K14, KK, 14.0, A.is_equal)
+        ts(E16, KK, 16.0, A.mult)
+        ts(full("B14"), full("BLK"), KL, A.mult)
+
+    def const_b():
+        ts(full("SH1"), full("DB"), 1.0, A.is_equal)
+        ts(full("BF"), full("BLK"), KL, A.mult)
+        ts(full("S0"), full("BLK"), K0, A.mult)
+        for i in range(2):
+            ts(("MK", 128 * i, 128 * i + 128), full("JM"), KK, A.is_equal)
+        ts(full("QF", 8), ("JI", 0, 8), GP, A.is_equal)
+        ts(full("QH", 8), ("JI", 0, 8), GP, A.is_equal)
+        ms(full("MN", 2048), 0.0)
+        op("v", g.vector.memset, dict(ap=T.MN[:, 0:2048:16], constant=512.0), [], [("MN", 0, 2048)])
+        ts(full("MB"), ("MK", 0, 128), P16, A.mult)
+        ts(full("NC0", 256), full("NF", 256), 0.0, A.add, K0, A.mult)
+        ts(full("PB", 16), full("PB0", 16), E16, A.add)
+
+    def const_c():
+        for t in range(1, 4):
+            ts(full("NC%d" % t, 256), full("NF", 256), 256.0 * t, A.add, K0, A.mult)
+        ts(full("SH2"), full("DB"), 2.0, A.is_equal)
+        ts(full("R14"), full("DIF"), 0.0, A.mult, K14, A.add)
+        ts(full("ROW1"), full("JM"), 1.0, A.is_equal)
+
+    def const_d():
+        ts(full("ROW0"), full("JM"), 0.0, A.is_equal)
+        ts(full("Q8", 8), ("JI", 0, 8), GP, A.is_equal, KL, A.mult)
+
+    for t in range(4):
+        for c in range(2):
+            arrives("m%d%d" % (t, c), -1, "MI%d%d" % (t, c), 0, 256)
+            arrives("y%d%d" % (t, c), 1 + t, "KI%d" % t, 128 * c, 128 * c + 128)
+            if t == 1:
+                arrives("h1%d" % c, -2, "HL1", 128 * c, 128 * c + 128)
+            if t >= 2:
+                arrives("h%d%d" % (t, c), -2, "HB%d" % t, 128 * c, 128 * c + 128)
+        arrives("v%d" % t, -1 - t, "VI%d" % t, 0, 512)
+    for c in range(2):
+        arrives("h0%d" % c, -4, "HL3", 128 * c, 128 * c + 128)
+        arrives("w%d" % c, 4, "L3I", 128 * c, 128 * c + 128)
+        arrives("m4%d" % c, 4, "MI4%d" % c, 0, 256)
+
+    def pre_u(t, c):
+        z, l, pz = ("MI%d%d" % (t, c), 0, 128), ("MI%d%d" % (t, c), 128, 256), "pZ%d" % c
+        u, um = ("pU", 0, 128), ("pU", 128, 256)
+        mm(u, full("WB"), z, True, False)
+        mm(u, full("CU"), full("ONE"), False, True)
+        act(full("U1%d" % c), u, F.Identity, bias=M35)
+        act(full("U2%d" % c), full("U1%d" % c), F.Identity, bias=-M35)
+        mm((pz, 0, 128), full("IH"), z, True, True)
+        mm((pz, 128, 256), full("DLM"), l, True, True)
+        mm(um, full("WB"), z, True, False)
+        mm(um, full("C32"), full("ONE"), False, False)
+        mm(um, full("NIB"), full("U2%d" % c), False, True)
+        if t < TURNS - 1:
+            mm(("pU", 256, 384), z, full("WB"), True, True)
+
+    def pre_v(t, c):
+        tt(full("AT%d" % c), ("MI%d%d" % (t, c), 128, 256), ("pU", 128, 256), A.mult)
+        ts(full("AS%d" % c), full("AT%d" % c), 5, A.arith_shift_right, 4095, A.bitwise_and)
+
+    def offs(t, c):
+        ts(full("OF%d" % c), full("AS%d" % c), K37 if t == 0 else AK, A.add)
+
+    def place_u(t, c):
+        if t < TURNS - 1:
+            tt(full("ZU%d" % c), ("pU", 256, 384), ("MK", 0, 128), A.mult)
+            mm(("pU", 400 + 8 * c, 408 + 8 * c), full("ZU%d" % c), full("QF", 8), True, True)
+
+    def place(t):
+        tc(full("PLI", 16), ("pU", 400, 416))
+        ts(full("PLA", 16), full("PLI", 16), 15, A.bitwise_and)
+        tt(full("PLB", 16), full("PLA", 16), full("PB", 16), A.add)
+        tc(full("PL", 16), full("PLB", 16))
+
+    def gather(c, a, b, q):
+        if a >= b:
+            return
+        y, of, w = ("Y%d" % c, 16 * a, 16 * b), ("OF%d" % c, a, b), ("RT", 0, RW)
+        if q == "s":
+            acti(y, w, of, F.Copy, scale=0.5)
+        else:
+            op("v", g.vector.tensor_scalar, dict(out=ap(y), in0=ind(w, of), scalar1=0.5, scalar2=None, op0=A.mult), [w, rg(of)], [rg(y)])
+
+    def compare_s(t, c):
+        y, b, z = "Y%d" % c, "B%d" % c, ("MI%d%d" % (t, c), 0, 128)
+        for i, k0 in enumerate(range(KS[c], 16, 4)):
+            k1 = min(k0 + 4, 16)
+            pd = "pD%d" % (i % 2)
+            for k in range(k0, k1):
+                o = (pd, 128 * (k - k0), 128 * (k - k0) + 128)
+                mm(o, full("IB"), (y, k, 2048, 16), True, False)
+                mm(o, full("NH"), z, False, True)
+            act((b, 128 * k0, 128 * k1), (pd, 0, 128 * (k1 - k0)), F.Sign, bias=-0.25)
+
+    def compare_v(t, c):
+        for k in range(KS[c]):
+            tt(("B%d" % c, 128 * k, 128 * k + 128), ("Y%d" % c, k, 2048, 16), ("pZ%d" % c, 0, 128), A.is_gt)
+
+    def beats(c):
+        mm(("pC", 0, 128), full("ONE"), full("C8%d" % c), True, False)
+        for k in range(16):
+            mm(("pC", k, 128, 16), ("B%d" % c, 128 * k, 128 * k + 128), full("QB" if k < KS[c] else "QBH", 8), False, k == 15)
+
+    def scan(c, hi):
+        o, y = full(("HI%d" if hi else "LO%d") % c, 2048), full("Y%d" % c, 2048)
+        m = full("MX" if hi else "MN", 2048)
+        op("v", g.vector.tensor_tensor_scan, dict(out=ap(o), data0=ap(m), data1=ap(y), initial=0.0,
+                                                  op0=A.mult if hi else A.add, op1=A.max if hi else A.min), [m, rg(y)], [rg(o)])
+
+    def verdict_v(c):
+        o, m = full("CM%d" % c), full("MX")
+        op("v", g.vector.tensor_tensor_scan, dict(out=ap(o), data0=ap(m), data1=ap(("pC", 0, 128)), initial=0.0, op0=A.mult, op1=A.max),
+           [m, ("pC", 0, 128)], [rg(o)])
+        ts(full("RN%d" % c), o, 10.5, A.is_lt)
+        mm(("pC", 128, 256), full("RN%d" % c), full("IB"), True, True)
+
+    def verdict_s(t, c):
+        run = ("RUN%d" % t, 128 * c, 128 * c + 128)
+        act(run, ("pC", 128, 256), F.Copy, accum=full("ACC%d" % c, 1))
+        mm(("pR", 128, 256), run, full("B14"), True, True)
+
+    def named(t, c):
+        run = ("RUN%d" % t, 128 * c, 128 * c + 128)
+        tt(full("P%d" % c), run, ("pZ%d" % c, 128, 256), A.mult)
+        mm(("pR", 0, 128), ("MI%d%d" % (t, c), 128, 256), full("S0"), True, False)
+        mm(("pR", 0, 128), full("P%d" % c), full("BF"), False, True)
+
+    def lists(t, c):
+        zm = "ZM%d" % c
+        tt(full(zm, 256), ("pR", 0, 256), full("MK", 256), A.mult)
+        mm(("pR", 256, 264), (zm, 0, 128), full("QH", 8), True, True)
+        mm(("pR", 264, 272), (zm, 128, 256), full("QH", 8), True, False)
+        mm(("pR", 264, 272), full("MB"), full("QH", 8), False, True)
+
+    def lists_out(t, c):
+        tc(full("LS%d" % c, 16), ("pR", 256, 272))
+
+    def select_hi(t, c):
+        acti(full("HG%d" % c), full("HI%d" % c, 2048), ("LS%d" % c, 8, 16), F.Identity, bias=-0.25)
+
+    def select(t, c):
+        kap, nam = ("LS%d" % c, 8, 16), ("LS%d" % c, 0, 8)
+        mo = "MO%d%d" % (t + 1, c)
+        tti((mo, 128, 256), full("TAB%d" % t, 512 + 256 * t), nam, ("NC%d" % t, 128 * c, 128 * c + 128), A.add)
+        tti(full("SM%d" % c), full("LO%d" % c, 2048), kap, full("HG%d" % c), A.add)
+        ts((mo, 0, 128), full("SM%d" % c), M23, A.add, M23, A.subtract)
+        send("m%d%d" % (t + 1, c), mo, 0, 256)
+        if t < 2:
+            send("h%d%d" % (t + 2, c), mo, 128, 256)
+
+    def update(t, c):
+        win, off = ("RT", 2048 * c, 2048 * c + 2048), ("PL", 8 * c, 8 * c + 8)
+        tti(full("RY%d" % c), win, off, ("MO%d%d" % (t + 1, c), 0, 128), A.add)
+        ts(full("RZ%d" % c), full("RY%d" % c), 1, A.arith_shift_right)
+        op("v", g.vector.tensor_copy, dict(out=ind(win, off), in_=ap(full("RZ%d" % c))), [off, rg(full("RZ%d" % c))], [win])
+        if c == 0:
+            dma("d", T.RT[:, 4096:RW], T.RT[:, 0:RW - 4096], [("RT", 0, RW - 4096)], [("RT", 4096, RW)])
+
+    def count():
+        for c in range(2):
+            mm(("pC", 256, 257), full("R14"), full("ACC%d" % c, 1), c == 0, c == 1)
+        ts(full("AI", 1), ("pC", 256, 257), -1.0, A.mult)
+        ts(full("AJ", 1), full("AI", 1), 255, A.bitwise_and)
+        ts(AK, full("AJ", 1), K37, A.add)
+
+    parts = {(0, 0): [(0, 0, "VI0", 1, 0)], (0, 1): [(1, 0, "VI1", 1, 0)], (1, 0): [(1, 512, "HL1", 2, 0)], (1, 1): [(2, 0, "VI2", 1, 0)],
+             (2, 0): [(2, 512, "HB2", 1, 0), (2, 768, "HB2", 2, 1)], (2, 1): [(3, 0, "VI3", 1, 0)],
+             (3, 0): [(3, 512, "HL3", 2, 0), (3, 768, "HB3", 1, 0)], (3, -1): [(3, 1024, "HB3", 2, 2)]}
+
+    def table_t(key):
+        a = 0
+        for tb, c0, src, sh, n in parts.get(key, []):
+            wd = 512 if src[0] == "V" else 256
+            w = ("pW", a, a + wd)
+            mm(w, full("SH%d" % sh), full(src, wd), True, sh == 1)
+            if sh == 2:
+                mm1(w, full("ROW1"), full("NC%d" % n, 256), False, True)
+            a += wd
+
+    def table_s(key):
+        a = 0
+        for tb, c0, src, sh, n in parts.get(key, []):
+            wd = 512 if src[0] == "V" else 256
+            act(("TAB%d" % tb, c0, c0 + wd), ("pW", a, a + wd), F.Copy)
+            a += wd
+
+    def run_out(t, c):
+        send("y%d%d" % (t, c), "RUN%d" % t, 128 * c, 128 * c + 128)
+
+    def turn(t):
+        last = t == TURNS - 1
+        offs(t, 0)
+        gather(0, 0, GS[0], "s")
+        gather(0, GS[0], H, "v")
+        if t == 0:
+            const_a()
+        compare_s(t, 0)
+        compare_v(t, 0)
+        if t == 0:
+            const_b()
+        place_u(t, 0)
+        pre_u(t, 1)
+        beats(0)
+        if last:
+            table_t((3, -1))
+            table_s((3, -1))
+        table_t((t, 0))
+        table_s((t, 0))
+        pre_v(t, 1)
+        offs(t, 1)
+        gather(1, 0, CUTS[0], "s")
+        verdict_v(0)
+        place_u(t, 1)
+        scan(0, True)
+        verdict_s(t, 0)
+        named(t, 0)
+        gather(1, CUTS[0], CUTS[1], "s")
+        scan(0, False)
+        lists(t, 0)
+        lists_out(t, 0)
+        if t == 0:
+            const_c()
+        if not last:
+            place(t)
+        select_hi(t, 0)
+        select(t, 0)
+        run_out(t, 0)
+        gather(1, CUTS[1], GS[1], "s")
+        gather(1, GS[1], H, "v")
+        if t == 0:
+            const_d()
+        if last:
+            for c in range(2):
+                send("w%d" % c, "MI3%d" % c, 128, 256)
+        table_t((t, 1))
+        compare_s(t, 1)
+        table_s((t, 1))
+        compare_v(t, 1)
+        beats(1)
+        if not last:
+            update(t, 0)
+        verdict_v(1)
+        scan(1, True)
+        verdict_s(t, 1)
+        named(t, 1)
+        scan(1, False)
+        lists(t, 1)
+        lists_out(t, 1)
+        select_hi(t, 1)
+        if not last:
+            pre_u(t + 1, 0)
+            count()
+        select(t, 1)
+        run_out(t, 1)
+        if not last:
+            update(t, 1)
+            pre_v(t + 1, 0)
+
+    pre_u(0, 0)
+    pre_v(0, 0)
+    for t in range(TURNS):
+        turn(t)
+
+    for t in range(TURNS):
+        w = T.pW[0:8, 0:256]
+        op("t", g.tensor.matmul, dict(out=w, lhsT=T.Q8[:], rhs=T["KI%d" % t][:], start=True, stop=True),
+           [full("Q8", 8), full("KI%d" % t, 256)], [("pW", 0, 256)])
+        op("s", g.scalar.activation, dict(out=T.YKS[:, 256 * t:256 * t + 256], in_=w, func=F.Copy), [("pW", 0, 256)], [("YKS", 256 * t, 256 * t + 256)])
+        if t == 2:
+            dma("d", T.yk[:, 0:768], T.YKS[:, 0:768], [("YKS", 0, 768)], [("yk", 0, 768)])
+            mm(("pC", 0, 256), full("SH1"), full("L3I", 256), True, False)
+            mm1(("pC", 0, 256), full("ROW0"), full("NC3", 256), False, True)
+            act(full("YOS", 256), ("pC", 0, 256), F.Copy)
+            dma("d", T.yo[:], T.YOS[:], [full("YOS", 256)], [("yo", 0, 256)])
+    for c in range(2):
+        a, b = 128 * c, 128 * c + 128
+        tc(("YPS", a, b), ("MI4%d" % c, 128, 256))
+        dma("d", T.yp[:, a:b], T.YPS[:, a:b], [("YPS", a, b)], [("yp", a, b)])
+        tc(("YZS", a, b), ("MI4%d" % c, 0, 128))
+        dma("d", T.yz[:, a:b], T.YZS[:, a:b], [("YZS", a, b)], [("yz", a, b)])
+    dma("d", T.yk[:, 768:1024], T.YKS[:, 768:1024], [("YKS", 768, 1024)], [("yk", 768, 1024)])
+    used["ls"] = state["ls"]
+    for s in sorted(used):
+        if known["g"].get(s, 0) < used[s]:
+            g.wait_ge(T.sem[s], used[s])

@@ -2,9 +2,9 @@ from concourse.mybir import AluOpType as A, ActivationFunctionType as F
 
 N, TURNS, H = 8, 4, 128
 RW = 4096 + 816
-GS = (64, 128)
-CUTS = (48, 88)
-KS = (9, 8)
+GS = (64, 96)
+CUTS = (56, 96)
+KS = (9, 7)
 M35, M23 = 1.5 * 2.0 ** 35, 1.5 * 2.0 ** 23
 
 SCRATCH = {
@@ -406,25 +406,19 @@ def rank_program(g, core, T, topo):
         mm(um, full("C32"), full("ONE"), False, False)
         mm(um, full("NIB"), full("U2%d" % c), False, True)
         if t < TURNS - 1:
-            mm(("pU", 256, 384), z, full("WB"), True, True)
-
-    def pre_v(t, c):
-        tt(full("AT%d" % c), ("MI%d%d" % (t, c), 128, 256), ("pU", 128, 256), A.mult)
-        ts(full("AS%d" % c), full("AT%d" % c), 5, A.arith_shift_right, 4095, A.bitwise_and)
+            mm((pz, 256, 384), z, full("WB"), True, True)
 
     def offs(t, c):
         ts(full("OF%d" % c), full("AS%d" % c), K37 if t == 0 else AK, A.add)
 
     def place_u(t, c):
         if t < TURNS - 1:
-            tt(full("ZU%d" % c), ("pU", 256, 384), ("MK", 0, 128), A.mult)
+            tt(full("ZU%d" % c), ("pZ%d" % c, 256, 384), ("MK", 0, 128), A.mult)
             mm(("pU", 400 + 8 * c, 408 + 8 * c), full("ZU%d" % c), full("QF", 8), True, True)
 
-    def place(t):
-        tc(full("PLI", 16), ("pU", 400, 416))
-        ts(full("PLA", 16), full("PLI", 16), 15, A.bitwise_and)
-        tt(full("PLB", 16), full("PLA", 16), full("PB", 16), A.add)
-        tc(full("PL", 16), full("PLB", 16))
+    def place_steps():
+        return [lambda: tc(full("PLI", 16), ("pU", 400, 416)), lambda: ts(full("PLA", 16), full("PLI", 16), 15, A.bitwise_and),
+                lambda: tt(full("PLB", 16), full("PLA", 16), full("PB", 16), A.add), lambda: tc(full("PL", 16), full("PLB", 16))]
 
     def gather(c, a, b, q):
         if a >= b:
@@ -492,34 +486,51 @@ def rank_program(g, core, T, topo):
     def select_hi(t, c):
         acti(full("HG%d" % c), full("HI%d" % c, 2048), ("LS%d" % c, 8, 16), F.Identity, bias=-0.25)
 
-    def select(t, c):
+    def select_steps(t, c):
         kap, nam = ("LS%d" % c, 8, 16), ("LS%d" % c, 0, 8)
         mo = "MO%d%d" % (t + 1, c)
-        tti((mo, 128, 256), full("TAB%d" % t, 512 + 256 * t), nam, ("NC%d" % t, 128 * c, 128 * c + 128), A.add)
-        tti(full("SM%d" % c), full("LO%d" % c, 2048), kap, full("HG%d" % c), A.add)
-        ts((mo, 0, 128), full("SM%d" % c), M23, A.add, M23, A.subtract)
-        send("m%d%d" % (t + 1, c), mo, 0, 256)
-        if t < 2:
-            send("h%d%d" % (t + 2, c), mo, 128, 256)
 
-    def update(t, c):
+        def out():
+            ts((mo, 0, 128), full("SM%d" % c), M23, A.add, M23, A.subtract)
+            send("m%d%d" % (t + 1, c), mo, 0, 256)
+            if t < 2:
+                send("h%d%d" % (t + 2, c), mo, 128, 256)
+        return [lambda: tti((mo, 128, 256), full("TAB%d" % t, 512 + 256 * t), nam, ("NC%d" % t, 128 * c, 128 * c + 128), A.add),
+                lambda: tti(full("SM%d" % c), full("LO%d" % c, 2048), kap, full("HG%d" % c), A.add), out]
+
+    def update_steps(t, c):
         win, off = ("RT", 2048 * c, 2048 * c + 2048), ("PL", 8 * c, 8 * c + 8)
-        tti(full("RY%d" % c), win, off, ("MO%d%d" % (t + 1, c), 0, 128), A.add)
-        ts(full("RZ%d" % c), full("RY%d" % c), 1, A.arith_shift_right)
-        op("v", g.vector.tensor_copy, dict(out=ind(win, off), in_=ap(full("RZ%d" % c))), [off, rg(full("RZ%d" % c))], [win])
-        if c == 0:
-            dma("d", T.RT[:, 4096:RW], T.RT[:, 0:RW - 4096], [("RT", 0, RW - 4096)], [("RT", 4096, RW)])
 
-    def count():
+        def out():
+            op("v", g.vector.tensor_copy, dict(out=ind(win, off), in_=ap(full("RZ%d" % c))), [off, rg(full("RZ%d" % c))], [win])
+            if c == 0:
+                act(("RT", 4096, RW), ("RT", 0, RW - 4096), F.Copy)
+        return [lambda: tti(full("RY%d" % c), win, off, ("MO%d%d" % (t + 1, c), 0, 128), A.add),
+                lambda: ts(full("RZ%d" % c), full("RY%d" % c), 1, A.arith_shift_right), out]
+
+    def count_t():
         for c in range(2):
             mm(("pC", 256, 257), full("R14"), full("ACC%d" % c, 1), c == 0, c == 1)
-        ts(full("AI", 1), ("pC", 256, 257), -1.0, A.mult)
-        ts(full("AJ", 1), full("AI", 1), 255, A.bitwise_and)
-        ts(AK, full("AJ", 1), K37, A.add)
 
-    parts = {(0, 0): [(0, 0, "VI0", 1, 0)], (0, 1): [(1, 0, "VI1", 1, 0)], (1, 0): [(1, 512, "HL1", 2, 0)], (1, 1): [(2, 0, "VI2", 1, 0)],
-             (2, 0): [(2, 512, "HB2", 1, 0), (2, 768, "HB2", 2, 1)], (2, 1): [(3, 0, "VI3", 1, 0)],
-             (3, 0): [(3, 512, "HL3", 2, 0), (3, 768, "HB3", 1, 0)], (3, -1): [(3, 1024, "HB3", 2, 2)]}
+    def count_steps():
+        return [lambda: ts(full("AI", 1), ("pC", 256, 257), -1.0, A.mult), lambda: ts(full("AJ", 1), full("AI", 1), 255, A.bitwise_and),
+                lambda: ts(AK, full("AJ", 1), K37, A.add)]
+
+    def pre_steps(t, c):
+        return [lambda: tt(full("AT%d" % c), ("MI%d%d" % (t, c), 128, 256), ("pU", 128, 256), A.mult),
+                lambda: ts(full("AS%d" % c), full("AT%d" % c), 5, A.arith_shift_right, 4095, A.bitwise_and), lambda: offs(t, c)]
+
+    def pre_v(t, c):
+        for f in pre_steps(t, c)[:2]:
+            f()
+
+    def select(t, c):
+        for f in select_steps(t, c):
+            f()
+
+    parts = {(0, 0): [(0, 0, "VI0", 1, 0)], (0, 1): [(1, 0, "VI1", 1, 0)], (1, 0): [(1, 512, "HL1", 2, 0), (3, 512, "HL3", 2, 0)],
+             (1, 1): [(2, 0, "VI2", 1, 0)], (2, 0): [(2, 512, "HB2", 1, 0), (2, 768, "HB2", 2, 1)], (2, 1): [(3, 0, "VI3", 1, 0)],
+             (3, 0): [(3, 768, "HB3", 1, 0), (3, 1024, "HB3", 2, 2)]}
 
     def table_t(key):
         a = 0
@@ -543,75 +554,84 @@ def rank_program(g, core, T, topo):
 
     def turn(t):
         last = t == TURNS - 1
-        offs(t, 0)
         gather(0, 0, GS[0], "s")
         gather(0, GS[0], H, "v")
         if t == 0:
             const_a()
         compare_s(t, 0)
+        pre_u(t, 1)
         compare_v(t, 0)
+        beats(0)
+        scan(0, True)
         if t == 0:
             const_b()
-        place_u(t, 0)
-        pre_u(t, 1)
-        beats(0)
-        if last:
-            table_t((3, -1))
-            table_s((3, -1))
-        table_t((t, 0))
-        table_s((t, 0))
+        scan(0, False)
         pre_v(t, 1)
         offs(t, 1)
         gather(1, 0, CUTS[0], "s")
+        gather(1, GS[1], H, "v")
+        table_t((t, 0))
         verdict_v(0)
-        place_u(t, 1)
-        scan(0, True)
+        place_u(t, 0)
         verdict_s(t, 0)
         named(t, 0)
         gather(1, CUTS[0], CUTS[1], "s")
-        scan(0, False)
+        table_s((t, 0))
         lists(t, 0)
+        place_u(t, 1)
         lists_out(t, 0)
+        select_hi(t, 0)
+        gather(1, CUTS[1], GS[1], "s")
         if t == 0:
             const_c()
-        if not last:
-            place(t)
-        select_hi(t, 0)
         select(t, 0)
         run_out(t, 0)
-        gather(1, CUTS[1], GS[1], "s")
-        gather(1, GS[1], H, "v")
-        if t == 0:
-            const_d()
         if last:
             for c in range(2):
                 send("w%d" % c, "MI3%d" % c, 128, 256)
-        table_t((t, 1))
         compare_s(t, 1)
-        table_s((t, 1))
         compare_v(t, 1)
         beats(1)
-        if not last:
-            update(t, 0)
-        verdict_v(1)
+        table_t((t, 1))
         scan(1, True)
-        verdict_s(t, 1)
-        named(t, 1)
+        if t == 0:
+            const_d()
         scan(1, False)
+        verdict_v(1)
+        verdict_s(t, 1)
+        pl = [] if last else place_steps()
+        for f in pl[:2]:
+            f()
+        named(t, 1)
+        table_s((t, 1))
+        for f in pl[2:]:
+            f()
         lists(t, 1)
+        if not last:
+            u0 = update_steps(t, 0)
+            u0[0]()
+            u0[1]()
         lists_out(t, 1)
         select_hi(t, 1)
-        if not last:
-            pre_u(t + 1, 0)
-            count()
-        select(t, 1)
+        if last:
+            select(t, 1)
+            run_out(t, 1)
+            return
+        count_t()
+        pre_u(t + 1, 0)
+        z = select_steps(t, 1)
+        u = update_steps(t, 1)
+        n = count_steps()
+        for f in (z[0], n[0], z[1], n[1], z[2], n[2], u0[2], u[0]):
+            f()
+        p = pre_steps(t + 1, 0)
+        for f in (p[0], u[1], p[1], u[2], p[2]):
+            f()
         run_out(t, 1)
-        if not last:
-            update(t, 1)
-            pre_v(t + 1, 0)
 
     pre_u(0, 0)
     pre_v(0, 0)
+    offs(0, 0)
     for t in range(TURNS):
         turn(t)
 

@@ -32,8 +32,9 @@ SCRATCH = {
     "PB0": ("sbuf", [128, 16], "int32"), "PLI": ("sbuf", [128, 16], "int32"), "PLA": ("sbuf", [128, 16], "int32"),
     "PLB": ("sbuf", [128, 16], "int32"), "PL": ("sbuf", [128, 16], "uint16"),
     "AI": ("sbuf", [128, 1], "int32"), "AJ": ("sbuf", [128, 1], "int32"),
-    "YKS": ("sbuf", [8, 1024], "float32"), "YPS": ("sbuf", [128, 256], "float32"), "YOS": ("sbuf", [128, 256], "float32"),
-    "YZS": ("sbuf", [128, 256], "bfloat16"),
+    "YKS": ("sbuf", [8, 1024], "float32"), "YOS": ("sbuf", [128, 256], "float32"),
+    "ZO": ("sbuf", [128, 256], "bfloat16"), "ZF": ("sbuf", [128, 256], "bfloat16"),
+    "EO": ("sbuf", [128, 256], "float32"), "EF": ("sbuf", [128, 256], "float32"),
     "pU": ("psum", [128, 512], "float32"), "pZ0": ("psum", [128, 512], "float32"), "pZ1": ("psum", [128, 512], "float32"),
     "pD0": ("psum", [128, 512], "float32"), "pD1": ("psum", [128, 512], "float32"), "pC": ("psum", [128, 512], "float32"),
     "pR": ("psum", [128, 512], "float32"), "pW": ("psum", [128, 512], "float32"),
@@ -62,7 +63,7 @@ for _n, _w, _d in (("Y", 2048, "bfloat16"), ("B", 2048, "bfloat16"), ("HI", 2048
 
 SEMAPHORES = (["qg", "qt", "qv", "qs", "ls"] + ["d%d" % i for i in range(28)]
               + ["m%d%d" % (t, c) for t in range(5) for c in range(2)] + ["v%d" % t for t in range(4)]
-              + ["h%d%d" % (t, c) for t in range(4) for c in range(2)] + ["y%d%d" % (t, c) for t in range(4) for c in range(2)] + ["w0", "w1"])
+              + ["h%d%d" % (t, c) for t in range(4) for c in range(2)] + ["y%d%d" % (t, c) for t in range(4) for c in range(2)] + ["w0", "w1", "z00", "z01", "e40", "e41"])
 
 
 def real(o):
@@ -93,7 +94,9 @@ def messages(core, T, topo):
         buf, a, b = real((buf, a, b))
         out.append((sem, dst, relay_of(core, dst, n, near, topo), buf, a, b))
     for c in range(2):
-        add("m0%d" % c, 1, "MI0%d" % c, 0, 256, c, True)
+        add("z0%d" % c, 1, "MI0%d" % c, 0, 128, c, True)
+    for c in range(2):
+        add("m0%d" % c, 1, "MI0%d" % c, 128, 256, c, True)
     add("v0", 1, "VI0", 0, 512, 0, False)
     add("v1", 2, "VI1", 0, 512, 0, False)
     add("v2", 3, "VI2", 0, 512, 1, False)
@@ -103,7 +106,11 @@ def messages(core, T, topo):
         add("h0%d" % c, 4, "HL3", 128 * c, 128 * c + 128, 0, False)
     for t in range(4):
         for c in range(2):
-            add("m%d%d" % (t + 1, c), 1 if t < 3 else -4, "MI%d%d" % (t + 1, c), 0, 256, c, True)
+            if t < 3:
+                add("m%d%d" % (t + 1, c), 1, "MI%d%d" % (t + 1, c), 0, 256, c, True)
+            else:
+                add("m4%d" % c, -4, "ZF", 128 * c, 128 * c + 128, 0, True)
+                add("e4%d" % c, -4, "EF", 128 * c, 128 * c + 128, 0, True)
             if t < 2:
                 add("h%d%d" % (t + 2, c), 2, "HB%d" % (t + 2), 128 * c, 128 * c + 128, 0, False)
             if t == 3:
@@ -287,10 +294,8 @@ def rank_program(g, core, T, topo):
     dma("d", T.VP32[:], T.vp[:], [], [("VP32", 0, 512)])
     dma("s", T.MV32[:], T.mv[:], [], [("MV32", 0, 16)])
     dma("s", T.Z0B[:], T.z0[:], [], [("Z0B", 0, 256)])
-    dma("d", T.VO32[:], T.vo[:], [], [("VO32", 0, 512)])
     dma("s", T.WT32[:], T.wt[:], [], [("WT32", 0, 1)])
-    dma("s", T.RT[:, 0:4096], T.strat[:], [], [("RT", 0, 4096)])
-    dma("d", T.RT[:, 4096:RW], T.strat[:, 0:RW - 4096], [], [("RT", 4096, RW)])
+    dma("d", T.RT[:, 0:4096], T.strat[:], [], [("RT", 0, 4096)])
 
     big = dict(allow_small_or_imprecise_dtypes=True)
     op("g", g.iota, dict(out=T.PI[:], pattern=[[0, 1]], base=0, channel_multiplier=1), [], [("PI", 0, 1)])
@@ -319,24 +324,26 @@ def rank_program(g, core, T, topo):
 
     tc(full("MV16", 16), full("MV32", 16))
     for c in range(2):
-        mo, off = "MO0%d" % c, ("MV16", 8 * c, 8 * c + 8)
+        mo = "MO0%d" % c
         tc((mo, 0, 128), ("Z0B", 128 * c, 128 * c + 128))
+        if c == 0:
+            send("z00", mo, 0, 128)
+    for c in range(2):
+        mo, off = "MO0%d" % c, ("MV16", 8 * c, 8 * c + 8)
         op("v", g.vector.tensor_copy, dict(out=ap((mo, 128, 256)), in_=ind(("VP32", 0, 512), off)), [("VP32", 0, 512), off], [rg((mo, 128, 256))])
-        send("m0%d" % c, mo, 0, 256)
+        send("m0%d" % c, mo, 128, 256)
+        if c == 0:
+            send("z01", "MO01", 0, 128)
+    dma("d", T.VO32[:], T.vo[:], [("MO", 384, 512)], [("VO32", 0, 512)])
     tt(full("DLM"), full("T0"), full("IB"), A.subtract)
     ts(full("NIB"), full("DIF"), 0.0, A.is_equal, -1.0, A.mult)
-    tc(full("OV", 512), full("VO32", 512))
-    send("v0", "OV", 0, 512)
     tc(full("WTF", 1), full("WT32", 1))
     ts(full("WB"), full("BLK"), full("WTF", 1), A.mult)
+    ms(full("MX", 2048), 1.0)
+    op("v", g.vector.memset, dict(ap=T.MX[:, 0:2048:16], constant=0.0), [], [("MX", 0, 2048)])
+    act(full("MN", 2048), full("MX", 2048), F.Identity, bias=512.0, scale=-512.0)
+    act(("RT", 4096, RW), ("RT", 0, RW - 4096), F.Copy)
     tc(full("PV", 512), full("VP32", 512))
-    send("v1", "PV", 0, 512)
-    for c in range(2):
-        send("h1%d" % c, "MO0%d" % c, 128, 256)
-    send("v2", "OV", 0, 512)
-    send("v3", "PV", 0, 512)
-    for c in range(2):
-        send("h0%d" % c, "MO0%d" % c, 128, 256)
 
     def const_a():
         ts(full("NH"), full("DIF"), 0.0, A.is_equal, -0.5, A.mult)
@@ -345,8 +352,6 @@ def rank_program(g, core, T, topo):
         ts(full("QBH", 8), ("JI", 0, 8), GP, A.is_equal, 0.5, A.mult)
         for c in range(2):
             ts(full("C8%d" % c), full("JM"), KS[c] - 0.5, A.is_gt, 0.0625, A.mult)
-        ms(full("MX", 2048), 1.0)
-        op("v", g.vector.memset, dict(ap=T.MX[:, 0:2048:16], constant=0.0), [], [("MX", 0, 2048)])
         ts(KL, KK, 15.0, A.is_lt)
         ts(K0, KK, 0.0, A.is_equal)
         ts(P16, full("PI", 1), 16.0, A.mult)
@@ -362,8 +367,6 @@ def rank_program(g, core, T, topo):
             ts(("MK", 128 * i, 128 * i + 128), full("JM"), KK, A.is_equal)
         ts(full("QF", 8), ("JI", 0, 8), GP, A.is_equal)
         ts(full("QH", 8), ("JI", 0, 8), GP, A.is_equal)
-        ms(full("MN", 2048), 0.0)
-        op("v", g.vector.memset, dict(ap=T.MN[:, 0:2048:16], constant=512.0), [], [("MN", 0, 2048)])
         ts(full("MB"), ("MK", 0, 128), P16, A.mult)
         ts(full("NC0", 256), full("NF", 256), 0.0, A.add, K0, A.mult)
         ts(full("PB", 16), full("PB0", 16), E16, A.add)
@@ -381,7 +384,7 @@ def rank_program(g, core, T, topo):
 
     for t in range(4):
         for c in range(2):
-            arrives("m%d%d" % (t, c), -1, "MI%d%d" % (t, c), 0, 256)
+            arrives("m%d%d" % (t, c), -1, "MI%d%d" % (t, c), 0 if t else 128, 256)
             arrives("y%d%d" % (t, c), 1 + t, "KI%d" % t, 128 * c, 128 * c + 128)
             if t == 1:
                 arrives("h1%d" % c, -2, "HL1", 128 * c, 128 * c + 128)
@@ -391,7 +394,9 @@ def rank_program(g, core, T, topo):
     for c in range(2):
         arrives("h0%d" % c, -4, "HL3", 128 * c, 128 * c + 128)
         arrives("w%d" % c, 4, "L3I", 128 * c, 128 * c + 128)
-        arrives("m4%d" % c, 4, "MI4%d" % c, 0, 256)
+        arrives("z0%d" % c, -1, "MI0%d" % c, 0, 128)
+        arrives("m4%d" % c, 4, "ZF", 128 * c, 128 * c + 128)
+        arrives("e4%d" % c, 4, "EF", 128 * c, 128 * c + 128)
 
     def pre_u(t, c):
         z, l, pz = ("MI%d%d" % (t, c), 0, 128), ("MI%d%d" % (t, c), 128, 256), "pZ%d" % c
@@ -489,14 +494,23 @@ def rank_program(g, core, T, topo):
     def select_steps(t, c):
         kap, nam = ("LS%d" % c, 8, 16), ("LS%d" % c, 0, 8)
         mo = "MO%d%d" % (t + 1, c)
+        half = (128 * c, 128 * c + 128)
+        z, l = ((mo, 0, 128), (mo, 128, 256)) if t < TURNS - 1 else (("ZO",) + half, ("EO",) + half)
+
+        def views():
+            tti(l, full("TAB%d" % t, 512 + 256 * t), nam, ("NC%d" % t,) + half, A.add)
+            if t == TURNS - 1:
+                send("e4%d" % c, *l)
 
         def out():
-            ts((mo, 0, 128), full("SM%d" % c), M23, A.add, M23, A.subtract)
+            ts(z, full("SM%d" % c), M23, A.add, M23, A.subtract)
+            if t == TURNS - 1:
+                send("m4%d" % c, *z)
+                return
             send("m%d%d" % (t + 1, c), mo, 0, 256)
             if t < 2:
-                send("h%d%d" % (t + 2, c), mo, 128, 256)
-        return [lambda: tti((mo, 128, 256), full("TAB%d" % t, 512 + 256 * t), nam, ("NC%d" % t, 128 * c, 128 * c + 128), A.add),
-                lambda: tti(full("SM%d" % c), full("LO%d" % c, 2048), kap, full("HG%d" % c), A.add), out]
+                send("h%d%d" % (t + 2, c), *l)
+        return [views, lambda: tti(full("SM%d" % c), full("LO%d" % c, 2048), kap, full("HG%d" % c), A.add), out]
 
     def update_steps(t, c):
         win, off = ("RT", 2048 * c, 2048 * c + 2048), ("PL", 8 * c, 8 * c + 8)
@@ -556,15 +570,11 @@ def rank_program(g, core, T, topo):
         last = t == TURNS - 1
         gather(0, 0, GS[0], "s")
         gather(0, GS[0], H, "v")
-        if t == 0:
-            const_a()
         compare_s(t, 0)
         pre_u(t, 1)
         compare_v(t, 0)
         beats(0)
         scan(0, True)
-        if t == 0:
-            const_b()
         scan(0, False)
         pre_v(t, 1)
         offs(t, 1)
@@ -582,8 +592,6 @@ def rank_program(g, core, T, topo):
         lists_out(t, 0)
         select_hi(t, 0)
         gather(1, CUTS[1], GS[1], "s")
-        if t == 0:
-            const_c()
         select(t, 0)
         run_out(t, 0)
         if last:
@@ -594,8 +602,6 @@ def rank_program(g, core, T, topo):
         beats(1)
         table_t((t, 1))
         scan(1, True)
-        if t == 0:
-            const_d()
         scan(1, False)
         verdict_v(1)
         verdict_s(t, 1)
@@ -614,8 +620,8 @@ def rank_program(g, core, T, topo):
         lists_out(t, 1)
         select_hi(t, 1)
         if last:
-            select(t, 1)
             run_out(t, 1)
+            select(t, 1)
             return
         count_t()
         pre_u(t + 1, 0)
@@ -629,6 +635,19 @@ def rank_program(g, core, T, topo):
             f()
         run_out(t, 1)
 
+    const_a()
+    const_b()
+    tc(full("OV", 512), full("VO32", 512))
+    send("v0", "OV", 0, 512)
+    send("v1", "PV", 0, 512)
+    for c in range(2):
+        send("h1%d" % c, "MO0%d" % c, 128, 256)
+    send("v2", "OV", 0, 512)
+    send("v3", "PV", 0, 512)
+    for c in range(2):
+        send("h0%d" % c, "MO0%d" % c, 128, 256)
+    const_c()
+    const_d()
     pre_u(0, 0)
     pre_v(0, 0)
     offs(0, 0)
@@ -646,13 +665,11 @@ def rank_program(g, core, T, topo):
             mm1(("pC", 0, 256), full("ROW0"), full("NC3", 256), False, True)
             act(full("YOS", 256), ("pC", 0, 256), F.Copy)
             dma("d", T.yo[:], T.YOS[:], [full("YOS", 256)], [("yo", 0, 256)])
+    dma("d", T.yk[:, 768:1024], T.YKS[:, 768:1024], [("YKS", 768, 1024)], [("yk", 768, 1024)])
     for c in range(2):
         a, b = 128 * c, 128 * c + 128
-        tc(("YPS", a, b), ("MI4%d" % c, 128, 256))
-        dma("d", T.yp[:, a:b], T.YPS[:, a:b], [("YPS", a, b)], [("yp", a, b)])
-        tc(("YZS", a, b), ("MI4%d" % c, 0, 128))
-        dma("d", T.yz[:, a:b], T.YZS[:, a:b], [("YZS", a, b)], [("yz", a, b)])
-    dma("d", T.yk[:, 768:1024], T.YKS[:, 768:1024], [("YKS", 768, 1024)], [("yk", 768, 1024)])
+        dma("d", T.yp[:, a:b], T.EF[:, a:b], [("EF", a, b)], [("yp", a, b)])
+        dma("s", T.yz[:, a:b], T.ZF[:, a:b], [("ZF", a, b)], [("yz", a, b)])
     used["ls"] = state["ls"]
     for s in sorted(used):
         if known["g"].get(s, 0) < used[s]:

from concourse.mybir import AluOpType as A, ActivationFunctionType as F

N, TURNS, H = 8, 4, 128
RW = 4096 + 816
GS = (64, 96)
CUTS = (56, 96)
KS = (9, 7)
M35, M23 = 1.5 * 2.0 ** 35, 1.5 * 2.0 ** 23

SCRATCH = {
    "RT": ("sbuf", [128, RW], "bfloat16"),
    "VP32": ("sbuf", [128, 512], "int32"), "VO32": ("sbuf", [128, 512], "int32"),
    "MV32": ("sbuf", [128, 16], "int32"), "MV16": ("sbuf", [128, 16], "uint16"),
    "Z0B": ("sbuf", [128, 256], "bfloat16"), "WT32": ("sbuf", [128, 1], "int32"), "WTF": ("sbuf", [128, 1], "float32"),
    "PV": ("sbuf", [128, 512], "float16"), "OV": ("sbuf", [128, 512], "float16"),
    "HL1": ("sbuf", [128, 256], "float16"), "HL3": ("sbuf", [128, 256], "float16"),
    "HB2": ("sbuf", [128, 256], "float16"), "HB3": ("sbuf", [128, 256], "float16"), "L3I": ("sbuf", [128, 256], "float16"),
    "MX": ("sbuf", [128, 2048], "bfloat16"), "MN": ("sbuf", [128, 2048], "bfloat16"),
    "DIF": ("sbuf", [128, 128], "float32"), "DB": ("sbuf", [128, 128], "float32"), "JI": ("sbuf", [128, 128], "int32"),
    "JS": ("sbuf", [128, 128], "int32"), "JM": ("sbuf", [128, 128], "int32"), "PI": ("sbuf", [128, 1], "int32"),
    "PG": ("sbuf", [128, 1], "int32"), "PK": ("sbuf", [128, 1], "int32"), "COL": ("sbuf", [128, 16], "float32"),
    "BLK": ("sbuf", [128, 128], "bfloat16"), "T0": ("sbuf", [128, 128], "bfloat16"), "T1": ("sbuf", [128, 128], "bfloat16"),
    "IB": ("sbuf", [128, 128], "bfloat16"), "NIB": ("sbuf", [128, 128], "bfloat16"), "IH": ("sbuf", [128, 128], "float16"),
    "NH": ("sbuf", [128, 128], "float16"), "B14": ("sbuf", [128, 128], "bfloat16"),
    "BF": ("sbuf", [128, 128], "float16"), "S0": ("sbuf", [128, 128], "float16"), "WB": ("sbuf", [128, 128], "float16"),
    "DLM": ("sbuf", [128, 128], "float16"), "SH1": ("sbuf", [128, 128], "float16"), "SH2": ("sbuf", [128, 128], "float16"),
    "MK": ("sbuf", [128, 256], "float16"), "MB": ("sbuf", [128, 128], "float16"), "QH": ("sbuf", [128, 8], "float16"),
    "QF": ("sbuf", [128, 8], "float32"), "QB": ("sbuf", [128, 8], "bfloat16"), "QBH": ("sbuf", [128, 8], "bfloat16"),
    "Q8": ("sbuf", [128, 8], "bfloat16"), "R14": ("sbuf", [128, 128], "float32"), "ROW0": ("sbuf", [128, 128], "float16"),
    "ROW1": ("sbuf", [128, 128], "float16"), "ONE": ("sbuf", [128, 128], "float16"), "C32": ("sbuf", [128, 128], "float16"),
    "CU": ("sbuf", [128, 128], "float16"), "NF": ("sbuf", [128, 256], "float32"), "PB": ("sbuf", [128, 16], "int32"),
    "PB0": ("sbuf", [128, 16], "int32"), "PLI": ("sbuf", [128, 16], "int32"), "PLA": ("sbuf", [128, 16], "int32"),
    "PLB": ("sbuf", [128, 16], "int32"), "PL": ("sbuf", [128, 16], "uint16"),
    "AI": ("sbuf", [128, 1], "int32"), "AJ": ("sbuf", [128, 1], "int32"),
    "YKS": ("sbuf", [8, 1024], "float32"), "YOS": ("sbuf", [128, 256], "float32"),
    "ZO": ("sbuf", [128, 256], "bfloat16"), "ZF": ("sbuf", [128, 256], "bfloat16"),
    "EO": ("sbuf", [128, 256], "float32"), "EF": ("sbuf", [128, 256], "float32"),
    "pU": ("psum", [128, 512], "float32"), "pZ0": ("psum", [128, 512], "float32"), "pZ1": ("psum", [128, 512], "float32"),
    "pD0": ("psum", [128, 512], "float32"), "pD1": ("psum", [128, 512], "float32"), "pC": ("psum", [128, 512], "float32"),
    "pR": ("psum", [128, 512], "float32"), "pW": ("psum", [128, 512], "float32"),
    "MI": ("sbuf", [128, 2560], "float16"),
    "MO": ("sbuf", [128, 2560], "float16"),
}
for _t in range(4):
    SCRATCH["VI%d" % _t] = ("sbuf", [128, 512], "float16")
    SCRATCH["TAB%d" % _t] = ("sbuf", [128, 512 + 256 * _t], "float32")
    SCRATCH["NC%d" % _t] = ("sbuf", [128, 256], "float16")
    SCRATCH["RUN%d" % _t] = ("sbuf", [128, 256], "bfloat16")
    SCRATCH["KI%d" % _t] = ("sbuf", [128, 256], "bfloat16")
ALIAS = {}
for _c in range(2):
    for _t in range(5):
        ALIAS["MI%d%d" % (_t, _c)] = ("MI", 256 * (2 * _t + _c))
        ALIAS["MO%d%d" % (_t, _c)] = ("MO", 256 * (2 * _t + _c))
for _n, _w, _d in (("Y", 2048, "bfloat16"), ("B", 2048, "bfloat16"), ("HI", 2048, "bfloat16"), ("LO", 2048, "bfloat16"),
                   ("U1", 128, "float32"), ("U2", 128, "bfloat16"), ("AT", 128, "int32"), ("AS", 128, "int32"), ("OF", 128, "uint16"),
                   ("CM", 128, "bfloat16"), ("RN", 128, "bfloat16"), ("P", 128, "float16"), ("ZM", 256, "float16"), ("ZU", 128, "float32"),
                   ("LS", 16, "uint16"), ("HG", 128, "float32"), ("SM", 128, "float32"), ("RY", 128, "int32"), ("RZ", 128, "int32"),
                   ("ACC", 1, "float32"), ("C8", 128, "float16")):
    SCRATCH[_n] = ("sbuf", [128, 2 * _w], _d)
    for _c in range(2):
        ALIAS["%s%d" % (_n, _c)] = (_n, _w * _c)

SEMAPHORES = (["qg", "qt", "qv", "qs", "ls"] + ["d%d" % i for i in range(28)]
              + ["m%d%d" % (t, c) for t in range(5) for c in range(2)] + ["v%d" % t for t in range(4)]
              + ["h%d%d" % (t, c) for t in range(4) for c in range(2)] + ["y%d%d" % (t, c) for t in range(4) for c in range(2)] + ["w0", "w1", "z00", "z01", "e40", "e41"])


def real(o):
    if o[0] in ALIAS:
        n, a = ALIAS[o[0]]
        return (n, o[1] + a, o[2] + a) + tuple(o[3:])
    return o


def bits(m):
    return bin(m).count("1")


def relay_of(src, dst, n, near, topo):
    if topo.may_write(src, dst):
        return None
    c = [x for x in topo.cores_of(src) if x != src and topo.may_write(x, dst)]
    c = [x for x in c if (topo.die(x) == topo.die(src)) == near]
    return c[n % len(c)]


def messages(core, T, topo):
    r = T.rank_of(core)
    out = []

    def add(sem, off, buf, a, b, n, near):
        dst = T.cores[(r + off) % N]
        buf, a, b = real((buf, a, b))
        out.append((sem, dst, relay_of(core, dst, n, near, topo), buf, a, b))
    for c in range(2):
        add("z0%d" % c, 1, "MI0%d" % c, 0, 128, c, True)
    for c in range(2):
        add("m0%d" % c, 1, "MI0%d" % c, 128, 256, c, True)
    add("v0", 1, "VI0", 0, 512, 0, False)
    add("v1", 2, "VI1", 0, 512, 0, False)
    add("v2", 3, "VI2", 0, 512, 1, False)
    add("v3", 4, "VI3", 0, 512, 0, False)
    for c in range(2):
        add("h1%d" % c, 2, "HL1", 128 * c, 128 * c + 128, 0, False)
        add("h0%d" % c, 4, "HL3", 128 * c, 128 * c + 128, 0, False)
    for t in range(4):
        for c in range(2):
            if t < 3:
                add("m%d%d" % (t + 1, c), 1, "MI%d%d" % (t + 1, c), 0, 256, c, True)
            else:
                add("m4%d" % c, -4, "ZF", 128 * c, 128 * c + 128, 0, True)
                add("e4%d" % c, -4, "EF", 128 * c, 128 * c + 128, 0, True)
            if t < 2:
                add("h%d%d" % (t + 2, c), 2, "HB%d" % (t + 2), 128 * c, 128 * c + 128, 0, False)
            if t == 3:
                add("w%d" % c, -4, "L3I", 128 * c, 128 * c + 128, 0, False)
            add("y%d%d" % (t, c), -1 - t, "KI%d" % t, 128 * c, 128 * c + 128, c, False)
    return out


def mask_of(src, dst, topo):
    return sum(1 << x for x in topo.engines(src, dst)[:8])


def hand_on(g, core, T, topo):
    own = [x for x in topo.cores_of(core) if T.rank_of(x) is not None]
    n = 0
    for rc in own:
        for sem, dst, rel, buf, a, b in messages(rc, T, topo):
            if rel == core:
                g.wait_ge(T.sem[sem], bits(mask_of(rc, core, topo)))
                m = mask_of(core, dst, topo)
                rid, pid = topo.addr(dst, core)
                g.remote_dma(T[buf][:, a:b], T[buf][:, a:b], T.sem[sem], T.sem.ls, pid, rid, m)
                n += bits(m)
    if n:
        g.wait_ge(T.sem.ls, n)


def rank_program(g, core, T, topo):
    rank = T.rank_of(core)
    if rank is None:
        hand_on(g, core, T, topo)
        return
    Q = {"g": g, "t": g.tensor, "v": g.vector, "s": g.scalar, "d": g.sync}
    cnt = {"g": 0, "t": 0, "v": 0, "s": 0}
    known = {q: {} for q in Q}
    acc, bank, used = {}, {}, {}
    state = {"d": 0, "ls": 0}

    def need(q, tok):
        sem, val, clk = tok
        k = known[q]
        if k.get(sem, 0) < val:
            Q[q].wait_ge(T.sem[sem], val)
            k[sem] = val
        for s2 in clk:
            if k.get(s2, 0) < clk[s2]:
                k[s2] = clk[s2]

    def deps(q, reads, writes):
        toks = []
        for w, lst in ((False, reads), (True, writes)):
            for nm, lo, hi in lst:
                if nm[0] == "p":
                    for q2 in bank.get(nm, {}):
                        if q2 != q:
                            toks.append(bank[nm][q2])
                    continue
                for lo2, hi2, w2, q2, tok in acc.get(nm, []):
                    if lo < hi2 and lo2 < hi and (w or w2) and not (q2 == q and w and not w2 and q in cnt):
                        toks.append(tok)
        best = {}
        for tok in toks:
            if tok[0] not in best or best[tok[0]][1] < tok[1]:
                best[tok[0]] = tok
        for tok in sorted(best.values(), key=lambda x: -len(x[2])):
            need(q, tok)

    def note(q, reads, writes, tok):
        for w, lst in ((False, reads), (True, writes)):
            for nm, lo, hi in lst:
                if nm[0] == "p":
                    bank.setdefault(nm, {})[q] = tok
                    continue
                l = acc.setdefault(nm, [])
                if w:
                    l[:] = [e for e in l if not (lo <= e[0] and e[1] <= hi)]
                l.append((lo, hi, w, q, tok))

    def op(q, fn, args, reads, writes):
        deps(q, reads, writes)
        fn(**args).then_inc(T.sem["q" + q], 1)
        cnt[q] += 1
        used["q" + q] = cnt[q]
        note(q, reads, writes, ("q" + q, cnt[q], dict(known[q])))

    def dma(q, out, in_, reads, writes):
        deps(q, reads, writes)
        s = "d%d" % state["d"]
        state["d"] += 1
        Q[q].dma_start(out, in_).then_inc(T.sem[s], 16)
        used[s] = 16
        note(q, reads, writes, (s, 16, dict(known[q])))

    def arrives(sem, src_off, buf, a, b):
        src = T.cores[(rank + src_off) % N]
        for s2, dst, rel, bf, _a, _b in messages(src, T, topo):
            if s2 == sem and dst == core:
                v = bits(mask_of(rel if rel is not None else src, core, topo))
                used[sem] = v
                note("x", [], [real((buf, a, b))], (sem, v, {}))

    plan = {m[0]: m for m in messages(core, T, topo)}

    def send(sem, buf, a, b):
        _, dst, rel, ob, oa, oe = plan[sem]
        buf, a, b = real((buf, a, b))
        deps("g", [(buf, a, b)], [])
        to = dst if rel is None else rel
        m = mask_of(core, to, topo)
        rid, pid = topo.addr(to, core)
        g.remote_dma(T[ob][:, oa:oe], T[buf][:, a:b], T.sem[sem], T.sem.ls, pid, rid, m)
        state["ls"] += bits(m)

    def ap(o):
        o = real(o)
        if len(o) == 4:
            return T[o[0]][:, o[1]:o[2]:o[3]]
        return T[o[0]][:, o[1]:o[2]]

    def rg(o):
        return real(o)[:3]

    def ind(win, off):
        return ap(win).indirect(ap(off))

    def full(n, w=128):
        return (n, 0, w)

    def mm(out, l, r, start, stop):
        op("t", g.tensor.matmul, dict(out=ap(out), lhsT=ap(l), rhs=ap(r), start=start, stop=stop), [rg(l), rg(r)], [rg(out)])

    def mm1(out, l, r, start, stop):
        op("t", g.tensor.matmul, dict(out=ap(out), lhsT=T[l[0]][0:1, l[1]:l[2]], rhs=T[r[0]][0:1, r[1]:r[2]], start=start, stop=stop), [rg(l), rg(r)], [rg(out)])

    def tt(out, a, b, o):
        op("v", g.vector.tensor_tensor, dict(out=ap(out), in0=ap(a), in1=ap(b), op=o), [rg(a), rg(b)], [rg(out)])

    def tti(out, win, off, b, o):
        op("v", g.vector.tensor_tensor, dict(out=ap(out), in0=ind(win, off), in1=ap(b), op=o), [rg(win), rg(off), rg(b)], [rg(out)])

    def ts(out, a, s1, o1, s2=None, o2=None):
        rd = [rg(a)]
        sc = []
        for s in (s1, s2):
            if isinstance(s, tuple):
                rd.append(rg(s))
                sc.append(ap(s))
            else:
                sc.append(s)
        d = dict(out=ap(out), in0=ap(a), scalar1=sc[0], scalar2=sc[1], op0=o1)
        if o2 is not None:
            d["op1"] = o2
        op("v", g.vector.tensor_scalar, d, rd, [rg(out)])

    def tc(out, a):
        op("v", g.vector.tensor_copy, dict(out=ap(out), in_=ap(a)), [rg(a)], [rg(out)])

    def ms(out, v):
        op("v", g.vector.memset, dict(ap=ap(out), constant=v), [], [rg(out)])

    def act(out, a, f, bias=None, scale=None, accum=None):
        d = dict(out=ap(out), in_=ap(a), func=f)
        wr = [rg(out)]
        if bias is not None:
            d["bias"] = bias
        if scale is not None:
            d["scale"] = scale
        if accum is not None:
            d["accum_out"] = ap(accum)
            wr.append(rg(accum))
        op("s", g.scalar.activation, d, [rg(a)], wr)

    def acti(out, win, off, f, bias=None, scale=None):
        d = dict(out=ap(out), in_=ind(win, off), func=f)
        if bias is not None:
            d["bias"] = bias
        if scale is not None:
            d["scale"] = scale
        op("s", g.scalar.activation, d, [rg(win), rg(off)], [rg(out)])

    dma("d", T.VP32[:], T.vp[:], [], [("VP32", 0, 512)])
    dma("s", T.MV32[:], T.mv[:], [], [("MV32", 0, 16)])
    dma("s", T.Z0B[:], T.z0[:], [], [("Z0B", 0, 256)])
    dma("s", T.WT32[:], T.wt[:], [], [("WT32", 0, 1)])
    dma("d", T.RT[:, 0:4096], T.strat[:], [], [("RT", 0, 4096)])

    big = dict(allow_small_or_imprecise_dtypes=True)
    op("g", g.iota, dict(out=T.PI[:], pattern=[[0, 1]], base=0, channel_multiplier=1), [], [("PI", 0, 1)])
    op("g", g.iota, dict(out=T.JI[:], pattern=[[1, 128]], base=0, channel_multiplier=0), [], [("JI", 0, 128)])
    op("g", g.iota, dict(out=T.DIF[:], pattern=[[1, 128]], base=0, channel_multiplier=-1, **big), [], [("DIF", 0, 128)])
    op("g", g.iota, dict(out=T.PB0[:], pattern=[[0, 2], [256, 8]], base=0, channel_multiplier=0), [], [("PB0", 0, 16)])
    op("g", g.iota, dict(out=T.NF[:], pattern=[[1, 256]], base=512, channel_multiplier=0, **big), [], [("NF", 0, 256)])

    GP, KK, P16, K0, K14, KL, K37, E16, AK = [("COL", i, i + 1) for i in range(9)]
    ts(full("PG", 1), full("PI", 1), 4, A.arith_shift_right)
    ts(full("PK", 1), full("PI", 1), 15, A.bitwise_and)
    ts(full("JS"), full("JI"), 4, A.arith_shift_right)
    tc(GP, full("PG", 1))
    tc(KK, full("PK", 1))
    ts(K37, KK, 37.0, A.mult)
    ts(full("BLK"), full("JS"), GP, A.is_equal)
    ts(full("IH"), full("DIF"), 0.0, A.is_equal, 0.5, A.mult)
    ts(full("T1"), full("BLK"), 1000.0, A.mult, 1000.0, A.subtract)
    ms(full("ONE"), 1.0)
    ms(full("C32"), 0.25)
    tt(full("DB"), full("DIF"), full("T1"), A.add)
    op("v", g.vector.memset, dict(ap=T.CU[0:64, :], constant=-32.0), [], [("CU", 0, 64)])
    op("v", g.vector.memset, dict(ap=T.CU[64:128, :], constant=0.0078125), [], [("CU", 64, 128)])
    ts(full("T0"), full("DB"), -1.0, A.is_equal)
    ts(full("IB"), full("DIF"), 0.0, A.is_equal)

    tc(full("MV16", 16), full("MV32", 16))
    for c in range(2):
        mo = "MO0%d" % c
        tc((mo, 0, 128), ("Z0B", 128 * c, 128 * c + 128))
        if c == 0:
            send("z00", mo, 0, 128)
    for c in range(2):
        mo, off = "MO0%d" % c, ("MV16", 8 * c, 8 * c + 8)
        op("v", g.vector.tensor_copy, dict(out=ap((mo, 128, 256)), in_=ind(("VP32", 0, 512), off)), [("VP32", 0, 512), off], [rg((mo, 128, 256))])
        send("m0%d" % c, mo, 128, 256)
        if c == 0:
            send("z01", "MO01", 0, 128)
    dma("d", T.VO32[:], T.vo[:], [("MO", 384, 512)], [("VO32", 0, 512)])
    tt(full("DLM"), full("T0"), full("IB"), A.subtract)
    ts(full("NIB"), full("DIF"), 0.0, A.is_equal, -1.0, A.mult)
    tc(full("WTF", 1), full("WT32", 1))
    ts(full("WB"), full("BLK"), full("WTF", 1), A.mult)
    ms(full("MX", 2048), 1.0)
    op("v", g.vector.memset, dict(ap=T.MX[:, 0:2048:16], constant=0.0), [], [("MX", 0, 2048)])
    act(full("MN", 2048), full("MX", 2048), F.Identity, bias=512.0, scale=-512.0)
    act(("RT", 4096, RW), ("RT", 0, RW - 4096), F.Copy)
    tc(full("PV", 512), full("VP32", 512))

    def const_a():
        ts(full("NH"), full("DIF"), 0.0, A.is_equal, -0.5, A.mult)
        ts(full("JM"), full("JI"), 15, A.bitwise_and)
        ts(full("QB", 8), ("JI", 0, 8), GP, A.is_equal)
        ts(full("QBH", 8), ("JI", 0, 8), GP, A.is_equal, 0.5, A.mult)
        for c in range(2):
            ts(full("C8%d" % c), full("JM"), KS[c] - 0.5, A.is_gt, 0.0625, A.mult)
        ts(KL, KK, 15.0, A.is_lt)
        ts(K0, KK, 0.0, A.is_equal)
        ts(P16, full("PI", 1), 16.0, A.mult)
        ts(K14, KK, 14.0, A.is_equal)
        ts(E16, KK, 16.0, A.mult)
        ts(full("B14"), full("BLK"), KL, A.mult)

    def const_b():
        ts(full("SH1"), full("DB"), 1.0, A.is_equal)
        ts(full("BF"), full("BLK"), KL, A.mult)
        ts(full("S0"), full("BLK"), K0, A.mult)
        for i in range(2):
            ts(("MK", 128 * i, 128 * i + 128), full("JM"), KK, A.is_equal)
        ts(full("QF", 8), ("JI", 0, 8), GP, A.is_equal)
        ts(full("QH", 8), ("JI", 0, 8), GP, A.is_equal)
        ts(full("MB"), ("MK", 0, 128), P16, A.mult)
        ts(full("NC0", 256), full("NF", 256), 0.0, A.add, K0, A.mult)
        ts(full("PB", 16), full("PB0", 16), E16, A.add)

    def const_c():
        for t in range(1, 4):
            ts(full("NC%d" % t, 256), full("NF", 256), 256.0 * t, A.add, K0, A.mult)
        ts(full("SH2"), full("DB"), 2.0, A.is_equal)
        ts(full("R14"), full("DIF"), 0.0, A.mult, K14, A.add)
        ts(full("ROW1"), full("JM"), 1.0, A.is_equal)

    def const_d():
        ts(full("ROW0"), full("JM"), 0.0, A.is_equal)
        ts(full("Q8", 8), ("JI", 0, 8), GP, A.is_equal, KL, A.mult)

    for t in range(4):
        for c in range(2):
            arrives("m%d%d" % (t, c), -1, "MI%d%d" % (t, c), 0 if t else 128, 256)
            arrives("y%d%d" % (t, c), 1 + t, "KI%d" % t, 128 * c, 128 * c + 128)
            if t == 1:
                arrives("h1%d" % c, -2, "HL1", 128 * c, 128 * c + 128)
            if t >= 2:
                arrives("h%d%d" % (t, c), -2, "HB%d" % t, 128 * c, 128 * c + 128)
        arrives("v%d" % t, -1 - t, "VI%d" % t, 0, 512)
    for c in range(2):
        arrives("h0%d" % c, -4, "HL3", 128 * c, 128 * c + 128)
        arrives("w%d" % c, 4, "L3I", 128 * c, 128 * c + 128)
        arrives("z0%d" % c, -1, "MI0%d" % c, 0, 128)
        arrives("m4%d" % c, 4, "ZF", 128 * c, 128 * c + 128)
        arrives("e4%d" % c, 4, "EF", 128 * c, 128 * c + 128)

    def pre_u(t, c):
        z, l, pz = ("MI%d%d" % (t, c), 0, 128), ("MI%d%d" % (t, c), 128, 256), "pZ%d" % c
        u, um = ("pU", 0, 128), ("pU", 128, 256)
        mm(u, full("WB"), z, True, False)
        mm(u, full("CU"), full("ONE"), False, True)
        act(full("U1%d" % c), u, F.Identity, bias=M35)
        act(full("U2%d" % c), full("U1%d" % c), F.Identity, bias=-M35)
        mm((pz, 0, 128), full("IH"), z, True, True)
        mm((pz, 128, 256), full("DLM"), l, True, True)
        mm(um, full("WB"), z, True, False)
        mm(um, full("C32"), full("ONE"), False, False)
        mm(um, full("NIB"), full("U2%d" % c), False, True)
        if t < TURNS - 1:
            mm((pz, 256, 384), z, full("WB"), True, True)

    def offs(t, c):
        ts(full("OF%d" % c), full("AS%d" % c), K37 if t == 0 else AK, A.add)

    def place_u(t, c):
        if t < TURNS - 1:
            tt(full("ZU%d" % c), ("pZ%d" % c, 256, 384), ("MK", 0, 128), A.mult)
            mm(("pU", 400 + 8 * c, 408 + 8 * c), full("ZU%d" % c), full("QF", 8), True, True)

    def place_steps():
        return [lambda: tc(full("PLI", 16), ("pU", 400, 416)), lambda: ts(full("PLA", 16), full("PLI", 16), 15, A.bitwise_and),
                lambda: tt(full("PLB", 16), full("PLA", 16), full("PB", 16), A.add), lambda: tc(full("PL", 16), full("PLB", 16))]

    def gather(c, a, b, q):
        if a >= b:
            return
        y, of, w = ("Y%d" % c, 16 * a, 16 * b), ("OF%d" % c, a, b), ("RT", 0, RW)
        if q == "s":
            acti(y, w, of, F.Copy, scale=0.5)
        else:
            op("v", g.vector.tensor_scalar, dict(out=ap(y), in0=ind(w, of), scalar1=0.5, scalar2=None, op0=A.mult), [w, rg(of)], [rg(y)])

    def compare_s(t, c):
        y, b, z = "Y%d" % c, "B%d" % c, ("MI%d%d" % (t, c), 0, 128)
        for i, k0 in enumerate(range(KS[c], 16, 4)):
            k1 = min(k0 + 4, 16)
            pd = "pD%d" % (i % 2)
            for k in range(k0, k1):
                o = (pd, 128 * (k - k0), 128 * (k - k0) + 128)
                mm(o, full("IB"), (y, k, 2048, 16), True, False)
                mm(o, full("NH"), z, False, True)
            act((b, 128 * k0, 128 * k1), (pd, 0, 128 * (k1 - k0)), F.Sign, bias=-0.25)

    def compare_v(t, c):
        for k in range(KS[c]):
            tt(("B%d" % c, 128 * k, 128 * k + 128), ("Y%d" % c, k, 2048, 16), ("pZ%d" % c, 0, 128), A.is_gt)

    def beats(c):
        mm(("pC", 0, 128), full("ONE"), full("C8%d" % c), True, False)
        for k in range(16):
            mm(("pC", k, 128, 16), ("B%d" % c, 128 * k, 128 * k + 128), full("QB" if k < KS[c] else "QBH", 8), False, k == 15)

    def scan(c, hi):
        o, y = full(("HI%d" if hi else "LO%d") % c, 2048), full("Y%d" % c, 2048)
        m = full("MX" if hi else "MN", 2048)
        op("v", g.vector.tensor_tensor_scan, dict(out=ap(o), data0=ap(m), data1=ap(y), initial=0.0,
                                                  op0=A.mult if hi else A.add, op1=A.max if hi else A.min), [m, rg(y)], [rg(o)])

    def verdict_v(c):
        o, m = full("CM%d" % c), full("MX")
        op("v", g.vector.tensor_tensor_scan, dict(out=ap(o), data0=ap(m), data1=ap(("pC", 0, 128)), initial=0.0, op0=A.mult, op1=A.max),
           [m, ("pC", 0, 128)], [rg(o)])
        ts(full("RN%d" % c), o, 10.5, A.is_lt)
        mm(("pC", 128, 256), full("RN%d" % c), full("IB"), True, True)

    def verdict_s(t, c):
        run = ("RUN%d" % t, 128 * c, 128 * c + 128)
        act(run, ("pC", 128, 256), F.Copy, accum=full("ACC%d" % c, 1))
        mm(("pR", 128, 256), run, full("B14"), True, True)

    def named(t, c):
        run = ("RUN%d" % t, 128 * c, 128 * c + 128)
        tt(full("P%d" % c), run, ("pZ%d" % c, 128, 256), A.mult)
        mm(("pR", 0, 128), ("MI%d%d" % (t, c), 128, 256), full("S0"), True, False)
        mm(("pR", 0, 128), full("P%d" % c), full("BF"), False, True)

    def lists(t, c):
        zm = "ZM%d" % c
        tt(full(zm, 256), ("pR", 0, 256), full("MK", 256), A.mult)
        mm(("pR", 256, 264), (zm, 0, 128), full("QH", 8), True, True)
        mm(("pR", 264, 272), (zm, 128, 256), full("QH", 8), True, False)
        mm(("pR", 264, 272), full("MB"), full("QH", 8), False, True)

    def lists_out(t, c):
        tc(full("LS%d" % c, 16), ("pR", 256, 272))

    def select_hi(t, c):
        acti(full("HG%d" % c), full("HI%d" % c, 2048), ("LS%d" % c, 8, 16), F.Identity, bias=-0.25)

    def select_steps(t, c):
        kap, nam = ("LS%d" % c, 8, 16), ("LS%d" % c, 0, 8)
        mo = "MO%d%d" % (t + 1, c)
        half = (128 * c, 128 * c + 128)
        z, l = ((mo, 0, 128), (mo, 128, 256)) if t < TURNS - 1 else (("ZO",) + half, ("EO",) + half)

        def views():
            tti(l, full("TAB%d" % t, 512 + 256 * t), nam, ("NC%d" % t,) + half, A.add)
            if t == TURNS - 1:
                send("e4%d" % c, *l)

        def out():
            ts(z, full("SM%d" % c), M23, A.add, M23, A.subtract)
            if t == TURNS - 1:
                send("m4%d" % c, *z)
                return
            send("m%d%d" % (t + 1, c), mo, 0, 256)
            if t < 2:
                send("h%d%d" % (t + 2, c), *l)
        return [views, lambda: tti(full("SM%d" % c), full("LO%d" % c, 2048), kap, full("HG%d" % c), A.add), out]

    def update_steps(t, c):
        win, off = ("RT", 2048 * c, 2048 * c + 2048), ("PL", 8 * c, 8 * c + 8)

        def out():
            op("v", g.vector.tensor_copy, dict(out=ind(win, off), in_=ap(full("RZ%d" % c))), [off, rg(full("RZ%d" % c))], [win])
            if c == 0:
                act(("RT", 4096, RW), ("RT", 0, RW - 4096), F.Copy)
        return [lambda: tti(full("RY%d" % c), win, off, ("MO%d%d" % (t + 1, c), 0, 128), A.add),
                lambda: ts(full("RZ%d" % c), full("RY%d" % c), 1, A.arith_shift_right), out]

    def count_t():
        for c in range(2):
            mm(("pC", 256, 257), full("R14"), full("ACC%d" % c, 1), c == 0, c == 1)

    def count_steps():
        return [lambda: ts(full("AI", 1), ("pC", 256, 257), -1.0, A.mult), lambda: ts(full("AJ", 1), full("AI", 1), 255, A.bitwise_and),
                lambda: ts(AK, full("AJ", 1), K37, A.add)]

    def pre_steps(t, c):
        return [lambda: tt(full("AT%d" % c), ("MI%d%d" % (t, c), 128, 256), ("pU", 128, 256), A.mult),
                lambda: ts(full("AS%d" % c), full("AT%d" % c), 5, A.arith_shift_right, 4095, A.bitwise_and), lambda: offs(t, c)]

    def pre_v(t, c):
        for f in pre_steps(t, c)[:2]:
            f()

    def select(t, c):
        for f in select_steps(t, c):
            f()

    parts = {(0, 0): [(0, 0, "VI0", 1, 0)], (0, 1): [(1, 0, "VI1", 1, 0)], (1, 0): [(1, 512, "HL1", 2, 0), (3, 512, "HL3", 2, 0)],
             (1, 1): [(2, 0, "VI2", 1, 0)], (2, 0): [(2, 512, "HB2", 1, 0), (2, 768, "HB2", 2, 1)], (2, 1): [(3, 0, "VI3", 1, 0)],
             (3, 0): [(3, 768, "HB3", 1, 0), (3, 1024, "HB3", 2, 2)]}

    def table_t(key):
        a = 0
        for tb, c0, src, sh, n in parts.get(key, []):
            wd = 512 if src[0] == "V" else 256
            w = ("pW", a, a + wd)
            mm(w, full("SH%d" % sh), full(src, wd), True, sh == 1)
            if sh == 2:
                mm1(w, full("ROW1"), full("NC%d" % n, 256), False, True)
            a += wd

    def table_s(key):
        a = 0
        for tb, c0, src, sh, n in parts.get(key, []):
            wd = 512 if src[0] == "V" else 256
            act(("TAB%d" % tb, c0, c0 + wd), ("pW", a, a + wd), F.Copy)
            a += wd

    def run_out(t, c):
        send("y%d%d" % (t, c), "RUN%d" % t, 128 * c, 128 * c + 128)

    def turn(t):
        last = t == TURNS - 1
        gather(0, 0, GS[0], "s")
        gather(0, GS[0], H, "v")
        compare_s(t, 0)
        pre_u(t, 1)
        compare_v(t, 0)
        beats(0)
        scan(0, True)
        scan(0, False)
        pre_v(t, 1)
        offs(t, 1)
        gather(1, 0, CUTS[0], "s")
        gather(1, GS[1], H, "v")
        table_t((t, 0))
        verdict_v(0)
        place_u(t, 0)
        verdict_s(t, 0)
        named(t, 0)
        gather(1, CUTS[0], CUTS[1], "s")
        table_s((t, 0))
        lists(t, 0)
        place_u(t, 1)
        lists_out(t, 0)
        select_hi(t, 0)
        gather(1, CUTS[1], GS[1], "s")
        select(t, 0)
        run_out(t, 0)
        if last:
            for c in range(2):
                send("w%d" % c, "MI3%d" % c, 128, 256)
        compare_s(t, 1)
        compare_v(t, 1)
        beats(1)
        table_t((t, 1))
        scan(1, True)
        scan(1, False)
        verdict_v(1)
        verdict_s(t, 1)
        pl = [] if last else place_steps()
        for f in pl[:2]:
            f()
        named(t, 1)
        table_s((t, 1))
        for f in pl[2:]:
            f()
        lists(t, 1)
        if not last:
            u0 = update_steps(t, 0)
            u0[0]()
            u0[1]()
        lists_out(t, 1)
        select_hi(t, 1)
        if last:
            run_out(t, 1)
            select(t, 1)
            return
        count_t()
        pre_u(t + 1, 0)
        z = select_steps(t, 1)
        u = update_steps(t, 1)
        n = count_steps()
        for f in (z[0], n[0], z[1], n[1], z[2], n[2], u0[2], u[0]):
            f()
        p = pre_steps(t + 1, 0)
        for f in (p[0], u[1], p[1], u[2], p[2]):
            f()
        run_out(t, 1)

    const_a()
    const_b()
    tc(full("OV", 512), full("VO32", 512))
    send("v0", "OV", 0, 512)
    send("v1", "PV", 0, 512)
    for c in range(2):
        send("h1%d" % c, "MO0%d" % c, 128, 256)
    send("v2", "OV", 0, 512)
    send("v3", "PV", 0, 512)
    for c in range(2):
        send("h0%d" % c, "MO0%d" % c, 128, 256)
    const_c()
    const_d()
    pre_u(0, 0)
    pre_v(0, 0)
    offs(0, 0)
    for t in range(TURNS):
        turn(t)

    for t in range(TURNS):
        w = T.pW[0:8, 0:256]
        op("t", g.tensor.matmul, dict(out=w, lhsT=T.Q8[:], rhs=T["KI%d" % t][:], start=True, stop=True),
           [full("Q8", 8), full("KI%d" % t, 256)], [("pW", 0, 256)])
        op("s", g.scalar.activation, dict(out=T.YKS[:, 256 * t:256 * t + 256], in_=w, func=F.Copy), [("pW", 0, 256)], [("YKS", 256 * t, 256 * t + 256)])
        if t == 2:
            dma("d", T.yk[:, 0:768], T.YKS[:, 0:768], [("YKS", 0, 768)], [("yk", 0, 768)])
            mm(("pC", 0, 256), full("SH1"), full("L3I", 256), True, False)
            mm1(("pC", 0, 256), full("ROW0"), full("NC3", 256), False, True)
            act(full("YOS", 256), ("pC", 0, 256), F.Copy)
            dma("d", T.yo[:], T.YOS[:], [full("YOS", 256)], [("yo", 0, 256)])
    dma("d", T.yk[:, 768:1024], T.YKS[:, 768:1024], [("YKS", 768, 1024)], [("yk", 768, 1024)])
    for c in range(2):
        a, b = 128 * c, 128 * c + 128
        dma("d", T.yp[:, a:b], T.EF[:, a:b], [("EF", a, b)], [("yp", a, b)])
        dma("s", T.yz[:, a:b], T.ZF[:, a:b], [("ZF", a, b)], [("yz", a, b)])
    used["ls"] = state["ls"]
    for s in sorted(used):
        if known["g"].get(s, 0) < used[s]:
            g.wait_ge(T.sem[s], used[s])
